import numpy as np
import ml_dtypes


def mxq(x, axis, fmt="e4m3"):
    dtype, down = {"e4m3": (ml_dtypes.float8_e4m3fn, 7), "e5m2": (ml_dtypes.float8_e5m2, 14)}[fmt]
    v = np.moveaxis(np.asarray(x, np.float32).astype(ml_dtypes.bfloat16).astype(np.float64), axis, -1)
    blocks = v.reshape(v.shape[:-1] + (-1, 32))
    amax = np.abs(blocks).max(-1, keepdims=True)
    byte = np.maximum(np.where(amax > 0, np.frexp(amax)[1] - 1 + 127, 0) - down, 1)
    scale = np.exp2(byte - 127.0)
    codes = (blocks / scale).astype(np.float32).astype(dtype).astype(np.float64)
    return np.moveaxis((codes * scale).reshape(v.shape), -1, axis)


WIDE = False


def mx_kscale(k):
    if not WIDE:
        return np.ones(k)
    levels = np.array([10, -10, 5, -5, 0])
    if k % 512:
        return np.exp2(np.random.permutation(np.resize(levels, k // 32))).repeat(32)
    a = np.empty((k // 512, 16))
    for p in range(k // 512):
        a[p, :8] = np.random.permutation(np.resize(levels, 8))
        for g in range(8):
            far = levels[np.abs(levels - a[p, g]) >= 10]
            a[p, g + 8] = far[np.random.randint(len(far))]
    return np.exp2(a.ravel()).repeat(32)


BF16 = ml_dtypes.bfloat16


def bf(x):
    return np.asarray(x, np.float32).astype(BF16)


def f64(x):
    return np.asarray(x).astype(np.float64)


E2M1 = np.array([0.0, 0.5, 1.0, 1.5, 2.0, 3.0, 4.0, 6.0, -0.0, -0.5, -1.0, -1.5, -2.0, -3.0, -4.0, -6.0])


def pack_weight(w, fmt):
    k, n = w.shape
    w = f64(bf(w)).reshape(k // 32, 32, n)
    amax = np.abs(w).max(1)
    if fmt == "e4m3":
        byte = np.frexp(amax)[1] - 1 + 127 - 7
    else:
        mant, ex = np.frexp(amax / 6.0)
        byte = np.where(mant > 0.5, ex, ex - 1) + 127
    byte = np.clip(np.where(amax > 0, byte, 1), 1, 254)
    scaled = (w * np.exp2(127.0 - byte)[:, None, :]).reshape(k, n).astype(np.float32)
    by_word = np.ascontiguousarray(scaled.reshape(k // 512, 128, 4, n).transpose(0, 1, 3, 2))
    if fmt == "e4m3":
        words = by_word.astype(ml_dtypes.float8_e4m3fn).view(np.uint8)
    else:
        c = by_word.astype(ml_dtypes.float4_e2m1fn).view(np.uint8) & 0xF
        words = c[..., 0::2] | (c[..., 1::2] << 4)
    return np.ascontiguousarray(words), np.ascontiguousarray(byte.astype(np.uint8).reshape(k // 512, 16, n))


def unpack_weight(words, scales, fmt):
    g, p, n, _ = words.shape
    if fmt == "e4m3":
        vals = np.ascontiguousarray(words).view(ml_dtypes.float8_e4m3fn).astype(np.float64)
    else:
        nib = np.empty((g, p, n, 4), np.uint8)
        nib[..., 0::2] = words & 0xF
        nib[..., 1::2] = words >> 4
        vals = E2M1[nib]
    vals = vals * np.repeat(np.exp2(scales.astype(np.float64) - 127.0), 8, axis=1)[..., None]
    return vals.transpose(0, 1, 3, 2).reshape(g * 512, n)
def pack4(w):
    words, scales = pack_weight(w, "e2m1")
    return words.reshape(words.shape[0], 128, -1), scales


def unpack4(words, scales):
    return unpack_weight(words.reshape(words.shape[0], 128, -1, 2), scales, "e2m1")


DL, D, DR, K, C = 256, 4, 256, 1536, 1024


def schmidt(count):
    return np.exp(0.3 * np.random.standard_normal(count) - np.arange(count) / count)


def draw0():
    s, u, t = mx_kscale(K), mx_kscale(K), mx_kscale(C)
    size = 2 / np.sqrt(K) / C ** 0.25
    x_words, x_scales = pack4(np.random.standard_normal((K, C)) * size / s[:, None] * t)
    return {"a": bf(np.random.standard_normal((DL, D, K)) * s),
            "x_words": x_words,
            "x_scales": x_scales,
            "y": bf(np.random.standard_normal((C, K)) * size * u / t[:, None]),
            "b": bf(np.random.standard_normal((K, D, DR)) / u[:, None, None]),
            "lam": bf(schmidt(C)),
            "lam_left": bf(schmidt(DL)),
            "lam_right": bf(schmidt(DR))}


def core(a, x_words, x_scales, y, b, lam, lam_left, lam_right):
    x = unpack4(x_words, x_scales)
    left = mxq(f64(a).reshape(DL * D, K), 1, "e4m3") @ x
    left = left * f64(lam)
    right = mxq(f64(y), 1, "e4m3") @ mxq(f64(b).reshape(K, D * DR), 0, "e4m3")
    theta = mxq(left, 1, "e4m3") @ mxq(right, 0, "e4m3")
    theta = theta.reshape(DL, D, D, DR) * f64(lam_left)[:, None, None, None]
    theta = theta * f64(lam_right)
    return theta.reshape(DL * D, D * DR)


def e4m3fn_bytes(y):
    return np.clip(np.asarray(y, np.float64), -448.0, 448.0).astype(np.float32).astype(ml_dtypes.float8_e4m3fn).view(np.uint8)


def e4m3fn_values(b):
    return np.asarray(b, np.uint8).view(ml_dtypes.float8_e4m3fn).astype(np.float64)


def setup_inputs():
    d = draw0()
    x0 = np.asarray(d['b']).astype(np.float64)
    s = (np.max(np.abs(x0), axis=(1, 2), keepdims=True) / 448.0).astype(np.float32)
    out = {}
    for k, v in d.items():
        if k == 'b':
            out['b_bytes'] = e4m3fn_bytes(x0 / s.astype(np.float64))
            out['b_scale'] = s
        else:
            out[k] = v
    return out


def reference(a, x_words, x_scales, y, b_bytes, b_scale, lam, lam_left, lam_right):
    return core(a, x_words, x_scales, y, e4m3fn_values(b_bytes) * b_scale.astype(np.float64), lam, lam_left, lam_right)

@@ -1,0 +1,344 @@
+from contextlib import ExitStack
+
+import concourse.mybir as mybir
+from concourse.masks import make_identity
+
+FLOPS = 2 * 1024 * 1536 * 1024 * 2 + 2 * 1024 * 1024 * 1024
+
+F32 = mybir.dt.float32
+BF16 = mybir.dt.bfloat16
+I32 = mybir.dt.int32
+U32 = mybir.dt.uint32
+U8 = mybir.dt.uint8
+FP8 = mybir.dt.float8_e4m3fn
+FP8X4 = mybir.dt.float8_e4m3fn_x4
+FP4X4 = mybir.dt.float4_e2m1fn_x4
+COPY = mybir.ActivationFunctionType.Copy
+MULT = mybir.AluOpType.mult
+
+P = 128
+G = 3
+H = 2
+
+
+def tile_two_site_tensor_s11_kernel(tc, a, x_words, x_scales, y, b_bytes, b_scale, lam, lam_left, lam_right, out):
+    nc = tc.nc
+    with ExitStack() as ctx:
+        keep = ctx.enter_context(tc.tile_pool(name="keep", bufs=1))
+        stream = ctx.enter_context(tc.tile_pool(name="stream", bufs=2))
+        psum = ctx.enter_context(tc.psum_pool(name="psum", bufs=2))
+        ctx.enter_context(tc.manual_schedule())
+
+        ident = keep.tile([P, P], F32, name="ident")
+        make_identity(nc, ident[:])
+        ident_y = keep.tile([P, 4, 32], F32, name="ident_y")
+        nc.gpsimd.tensor_copy(out=ident_y[:].rearrange("p t (q r) -> p t q r", r=8), in_=ident[:].rearrange("p (q t r) -> p t q r", q=4, t=4))
+        ident_bf = keep.tile([P, P], BF16, name="ident_bf")
+        make_identity(nc, ident_bf[:])
+        ones = keep.tile([P, P], BF16, name="ones")
+        nc.gpsimd.memset(ones[:], 1.0)
+        xs_raw = keep.tile([P, G, 256], I32, name="xs_raw")
+        nc.vector.memset(xs_raw[:], 0)
+        rows = keep.tile([P, P], BF16, name="rows")
+        nc.vector.memset(rows[:], 0.0)
+        right_row = keep.tile([P, 256], BF16, name="right_row")
+        nc.vector.memset(right_row[:], 0.0)
+
+        a_raw = {}
+        a_view = a.rearrange("(s p) e k -> s e p k", p=P)
+        y_raw = {}
+        y_view = y.rearrange("(h j p) k -> h j p k", h=H, p=P)
+
+        def load_a(s, e):
+            a_raw[s, e] = stream.tile([P, 1536], BF16, name="row_tile", bufs=12)
+            nc.sync.dma_start(out=a_raw[s, e][:], in_=a_view[s, e])
+
+        def load_y(h, t):
+            y_raw[h, t] = stream.tile([P, 1536], BF16, name="row_tile", bufs=12)
+            nc.sync.dma_start(out=y_raw[h, t][:], in_=y_view[h, t])
+
+        lam_view = lam.rearrange("(h q t r) -> h t q r", h=H, t=4, r=8)
+        b_cols = keep.tile([P, G, 4], F32, name="b_cols")
+        for h in range(H):
+            nc.scalar.dma_start(out=rows[4 * h : 4 * h + 4, :].rearrange("t (q r) -> t q r", r=8), in_=lam_view[h])
+        nc.scalar.dma_start(out=rows[8:10, :], in_=lam_left.rearrange("(s p) -> s p", p=P))
+        nc.scalar.dma_start(out=right_row[0:1, :], in_=lam_right.rearrange("(o j) -> o j", o=1))
+        nc.scalar.dma_start(out=b_cols[:], in_=b_scale.rearrange("(g p t) o u -> p g (t o u)", p=P, t=4))
+
+        for e in range(4):
+            load_a(0, e)
+        xs_view = x_scales.bitcast(I32).rearrange("g q w -> q g w")
+        for quad in range(4):
+            nc.sync.dma_start(out=xs_raw[32 * quad : 32 * quad + 4, :, :], in_=xs_view[4 * quad : 4 * quad + 4])
+        x_raw = keep.tile([P, G, 512], I32, name="x_raw")
+        nc.sync.dma_start(out=x_raw[:], in_=x_words.bitcast(I32).rearrange("g p w -> p g w"))
+        b_raw = keep.tile([P, G, 4096], U8, name="b_raw")
+        b_view = b_bytes.rearrange("(g p t) f j -> g p (t f j)", p=P, t=4)
+        for g in range(G):
+            nc.sync.dma_start(out=b_raw[:, g, :], in_=b_view[g])
+        for h in range(H):
+            for t in range(4):
+                load_y(h, t)
+        for e in range(4):
+            load_a(1, e)
+
+        x_codes = keep.tile([P, 4, G, H, 256], U8, name="x_codes", align_bytes=64)
+        x_plane = keep.tile([P, 4, G, H, 128], U8, name="x_plane", align_bytes=64)
+        codes = {}
+        planes = {}
+        for n in ("a0", "a1", "y0", "y1"):
+            codes[n] = keep.tile([P, G, 512], U32, name="codes_" + n, align_bytes=64)
+            planes[n] = keep.tile([P, G, 512], U8, name="planes_" + n, align_bytes=64)
+        for n in ("b0", "b1"):
+            codes[n] = keep.tile([P, G, 512], U32, name="codes_" + n, align_bytes=64)
+            planes[n] = keep.tile([P, G, 512], U8, name="planes_" + n, align_bytes=64)
+        for n in ("l0", "l1", "r0", "r1"):
+            codes[n] = keep.tile([P, H, 512], U32, name="codes_" + n, align_bytes=64)
+            planes[n] = keep.tile([P, H, 512], U8, name="planes_" + n, align_bytes=64)
+
+        def copy_out(engine, out_ap, in_ap):
+            if engine == "S":
+                nc.scalar.copy(out=out_ap, in_=in_ap)
+            else:
+                nc.vector.tensor_copy(out=out_ap, in_=in_ap)
+
+        grouped = {}
+
+        def turn(n, raws, pair, g, engine):
+            if pair == 0:
+                grouped[n, g] = stream.tile([P, 2048], BF16, name="grouped", bufs=6, align_bytes=64)
+            acc = psum.tile([P, 2, 256], F32, name="turned", bufs=3)
+            for x in range(2):
+                words = raws[2 * pair + x][:].bitcast(F32)
+                for u in range(2):
+                    src = words[:, 256 * g + u : 256 * (g + 1) : 2]
+                    if n[0] == "a":
+                        nc.tensor.transpose(acc[:, u, 128 * x : 128 * (x + 1)], src, ident[:])
+                    else:
+                        nc.tensor.transpose(acc[:, u, :].rearrange("p (t x c) -> p x t c", t=4, x=2)[:, x], src, ident_y[:].rearrange("p t c -> p (t c)"))
+            dst = grouped[n, g][:].bitcast(F32)
+            if n[0] == "a":
+                dst = dst[:, 512 * pair : 512 * (pair + 1)].rearrange("p (c u) -> p c u", u=2)
+                copy_out(engine, dst, acc[:].rearrange("p u c -> p c u"))
+            else:
+                dst = dst.rearrange("p (t x c u) -> p x t c u", t=4, x=2, u=2)[:, pair]
+                copy_out(engine, dst, acc[:].rearrange("p u (t c) -> p t c u", t=4))
+
+        def quantize(n, c, tile_bf):
+            nc.vector.quantize_mx(out=codes[n][:, c, :].bitcast(FP8X4), scales=planes[n][:, c, :], in_=tile_bf[:])
+
+        def permute_x():
+            nc.vector.tensor_copy(
+                out=x_plane[:].rearrange("p t g h c -> p (t g h c)").bitcast(I32).rearrange("p (t c r) -> p t c r", t=4, r=2),
+                in_=xs_raw[:].rearrange("p g w -> p (g w)").rearrange("p (c t r) -> p t c r", t=4, r=2),
+            )
+            nc.vector.tensor_copy(
+                out=x_codes[:].rearrange("p t g h c -> p (t g h c)").bitcast(I32).rearrange("p (t c r) -> p t c r", t=4, r=4),
+                in_=x_raw[:].rearrange("p g w -> p (g w)").rearrange("p (c t r) -> p t c r", t=4, r=4),
+            )
+
+        wide = {}
+
+        def widen(g, t, engine):
+            if t == 0:
+                wide[g] = stream.tile([P, 4, 1024], BF16, name="wide", bufs=3, align_bytes=64)
+            src = b_raw[:, g, 1024 * t : 1024 * (t + 1)].bitcast(FP8)
+            if engine == "S":
+                nc.scalar.activation(out=wide[g][:, t, :], in_=src, func=COPY, scale=b_cols[:, g, t : t + 1])
+            else:
+                nc.vector.tensor_scalar(out=wide[g][:, t, :], in0=src, scalar1=b_cols[:, g, t : t + 1], scalar2=None, op0=MULT)
+
+        inter = {}
+
+        def interleave(key, src):
+            inter[key] = stream.tile([P, 512, 4], BF16, name="inter", bufs=4, align_bytes=64)
+            nc.vector.tensor_copy(out=inter[key][:], in_=src.rearrange("p t n -> p n t"))
+
+        def inter_flat(key):
+            return inter[key][:].rearrange("p n t -> p (n t)")
+
+        def b_inter(g, half):
+            interleave(("b", g, half), wide[g][:, :, 512 * half : 512 * (half + 1)])
+
+        def b_quant(g, half):
+            nc.vector.quantize_mx(out=codes["b%d" % half][:, g, :].bitcast(FP8X4), scales=planes["b%d" % half][:, g, :], in_=inter_flat(("b", g, half)))
+
+        l_acc = {}
+        l_wide = {}
+
+        def l_mm(s, h):
+            for t in range(4):
+                l_acc[t] = psum.tile([P, 512], F32, name="acc", bufs=5)
+            n = "a%d" % s
+            for g in range(G):
+                for t in range(4):
+                    nc.tensor.matmul_mx(
+                        out=l_acc[t][:],
+                        lhsT=x_codes[:, t, g, h, :].bitcast(FP4X4),
+                        lhsT_scale=x_plane[:, t, g, h, :],
+                        rhs=codes[n][:, g, :].bitcast(FP8X4),
+                        rhs_scale=planes[n][:, g, :],
+                        start=(g == 0),
+                        stop=(g == G - 1),
+                    )
+
+        def l_out(s, h, t, engine):
+            if t == 0:
+                l_wide[s, h] = stream.tile([P, 4, 512], BF16, name="l_wide", bufs=3, align_bytes=64)
+            scale = lam_cols[:, 4 * h + t : 4 * h + t + 1]
+            if engine == "S":
+                nc.scalar.activation(out=l_wide[s, h][:, t, :], in_=l_acc[t][:], func=COPY, scale=scale)
+            else:
+                nc.vector.tensor_scalar(out=l_wide[s, h][:, t, :], in0=l_acc[t][:], scalar1=scale, scalar2=None, op0=MULT)
+
+        def l_inter(s, h):
+            interleave(("l", s, h), l_wide[s, h][:])
+
+        def l_quant(s, h):
+            n = "l%d" % s
+            nc.vector.quantize_mx(out=codes[n][:, h, :].bitcast(FP8X4), scales=planes[n][:, h, :], in_=inter_flat(("l", s, h)))
+
+        r_group = {}
+
+        def r_mm(h, n, engine):
+            half, m = divmod(n, 4)
+            if m == 0:
+                r_group[h, half] = stream.tile([P, 512, 4], BF16, name="r_group", bufs=3, align_bytes=64)
+            acc = psum.tile([P, 4, 128], F32, name="acc", bufs=5)
+            yn, bn = "y%d" % h, "b%d" % half
+            for t in range(4):
+                for g in range(G):
+                    nc.tensor.matmul_mx(
+                        out=acc[:, t, :],
+                        lhsT=codes[yn][:, g, 128 * t : 128 * (t + 1)].bitcast(FP8X4),
+                        lhsT_scale=planes[yn][:, g, 128 * t : 128 * (t + 1)],
+                        rhs=codes[bn][:, g, 128 * m : 128 * (m + 1)].bitcast(FP8X4),
+                        rhs_scale=planes[bn][:, g, 128 * m : 128 * (m + 1)],
+                        start=(g == 0),
+                        stop=(g == G - 1),
+                    )
+            copy_out(engine, r_group[h, half][:, 128 * m : 128 * (m + 1), :], acc[:].rearrange("p t n -> p n t"))
+
+        def r_quant(h, half):
+            n = "r%d" % half
+            nc.vector.quantize_mx(out=codes[n][:, h, :].bitcast(FP8X4), scales=planes[n][:, h, :], in_=r_group[h, half][:].rearrange("p n t -> p (n t)"))
+
+        out_view = out.rearrange("(s p e) n -> s e p n", p=P, e=4)
+
+        def theta(s, e, half):
+            acc = psum.tile([P, 512], F32, name="acc", bufs=5)
+            ln, rn = "l%d" % s, "r%d" % half
+            for h in range(H):
+                nc.tensor.matmul_mx(
+                    out=acc[:],
+                    lhsT=codes[ln][:, h, 128 * e : 128 * (e + 1)].bitcast(FP8X4),
+                    lhsT_scale=planes[ln][:, h, 128 * e : 128 * (e + 1)],
+                    rhs=codes[rn][:, h, :].bitcast(FP8X4),
+                    rhs_scale=planes[rn][:, h, :],
+                    start=(h == 0),
+                    stop=(h == H - 1),
+                )
+            o = stream.tile([P, 512], F32, name="o", bufs=6)
+            nc.vector.scalar_tensor_tensor(out=o[:], in0=acc[:], scalar=lam_cols[:, 8 + s : 9 + s], in1=right[:], op0=MULT, op1=MULT)
+            nc.sync.dma_start(out=out_view[s, e][:, 512 * half : 512 * (half + 1)], in_=o[:])
+
+        def raw_of(d, i):
+            return [d[i, j] for j in range(4)]
+
+        for g in range(G):
+            turn("a0", raw_of(a_raw, 0), 0, g, "VSV"[g])
+        for g in range(G):
+            turn("a0", raw_of(a_raw, 0), 1, g, "SVS"[g])
+        quantize("a0", 0, grouped["a0", 0])
+        permute_x()
+        quantize("a0", 1, grouped["a0", 1])
+        quantize("a0", 2, grouped["a0", 2])
+
+        lam_cols = keep.tile([P, 10], F32, name="lam_cols")
+        lam_ps = psum.tile([P, P], BF16, name="turned", bufs=3)
+        nc.tensor.transpose(lam_ps[:], rows[:], ident_bf[:])
+        nc.scalar.copy(out=lam_cols[:], in_=lam_ps[:, 0:10])
+        right = keep.tile([P, 512], F32, name="right")
+        right_ps = psum.tile([P, 2, 256], F32, name="acc", bufs=5)
+        for f in range(2):
+            nc.tensor.matmul(right_ps[:, f, :], lhsT=ones[:], rhs=right_row[:], start=True, stop=True)
+        nc.scalar.copy(out=right[:], in_=right_ps[:].rearrange("p f j -> p (f j)"))
+
+        for g in range(G):
+            for t in range(4):
+                widen(g, t, "S" if (g, t) in ((0, 0), (0, 1)) else "V")
+        l_mm(0, 0)
+        for t in range(4):
+            l_out(0, 0, t, "S")
+        l_mm(0, 1)
+        for t in range(4):
+            l_out(0, 1, t, "S")
+
+        for pair in range(2):
+            for g in range(G):
+                turn("y0", raw_of(y_raw, 0), pair, g, "S")
+        b_inter(0, 0)
+        b_inter(1, 0)
+        b_quant(0, 0)
+        b_inter(2, 0)
+        b_quant(1, 0)
+        quantize("y0", 0, grouped["y0", 0])
+        b_quant(2, 0)
+        quantize("y0", 1, grouped["y0", 1])
+        quantize("y0", 2, grouped["y0", 2])
+
+        for pair in range(2):
+            for g in range(G):
+                turn("y1", raw_of(y_raw, 1), pair, g, "S")
+        b_inter(0, 1)
+        quantize("y1", 0, grouped["y1", 0])
+        b_quant(0, 1)
+        quantize("y1", 1, grouped["y1", 1])
+        quantize("y1", 2, grouped["y1", 2])
+
+        for pair in range(2):
+            for g in range(G):
+                turn("a1", raw_of(a_raw, 1), pair, g, "S")
+        b_inter(1, 1)
+        quantize("a1", 0, grouped["a1", 0])
+        b_quant(1, 1)
+        quantize("a1", 1, grouped["a1", 1])
+        quantize("a1", 2, grouped["a1", 2])
+
+        for n in range(4):
+            r_mm(0, n, "S")
+        b_inter(2, 1)
+        l_inter(0, 0)
+        b_quant(2, 1)
+        l_quant(0, 0)
+        l_inter(0, 1)
+        for n in range(4):
+            r_mm(1, n, "S")
+        r_quant(0, 0)
+        l_quant(0, 1)
+        l_mm(1, 0)
+        r_quant(1, 0)
+        for t in range(4):
+            l_out(1, 0, t, "SVSV"[t])
+        l_mm(1, 1)
+        l_inter(1, 0)
+        for t in range(4):
+            l_out(1, 1, t, "SVSV"[t])
+        l_quant(1, 0)
+        for n in range(4, 8):
+            r_mm(0, n, "S")
+        l_inter(1, 1)
+        l_quant(1, 1)
+        for e in range(4):
+            theta(0, e, 0)
+        r_quant(0, 1)
+        for n in range(4, 8):
+            r_mm(1, n, "S")
+        for e in range(4):
+            theta(1, e, 0)
+            if e == 0:
+                r_quant(1, 1)
+        for e in range(4):
+            theta(0, e, 1)
+        for e in range(4):
+            theta(1, e, 1)

@@ -37,11 +37,13 @@ def tile_two_site_tensor_s11_kernel(tc, a, x_words, x_scales, y, b_bytes, b_scal
         make_identity(nc, ident_bf[:])
         ones = keep.tile([P, P], BF16, name="ones")
         nc.gpsimd.memset(ones[:], 1.0)
+        left_rows = keep.tile([P, P], BF16, name="left_rows")
+        right_row = keep.tile([P, 256], BF16, name="right_row")
         xs_raw = keep.tile([P, G, 256], I32, name="xs_raw")
         nc.vector.memset(xs_raw[:], 0)
         rows = keep.tile([P, P], BF16, name="rows")
         nc.vector.memset(rows[:], 0.0)
-        right_row = keep.tile([P, 256], BF16, name="right_row")
+        nc.vector.memset(left_rows[:], 0.0)
         nc.vector.memset(right_row[:], 0.0)
 
         a_raw = {}
@@ -50,28 +52,31 @@ def tile_two_site_tensor_s11_kernel(tc, a, x_words, x_scales, y, b_bytes, b_scal
         y_view = y.rearrange("(h j p) k -> h j p k", h=H, p=P)
 
         def load_a(s, e):
-            a_raw[s, e] = stream.tile([P, 1536], BF16, name="row_tile", bufs=12)
+            a_raw[s, e] = stream.tile([P, 1536], BF16, name="row_tile", bufs=10)
             nc.sync.dma_start(out=a_raw[s, e][:], in_=a_view[s, e])
 
         def load_y(h, t):
-            y_raw[h, t] = stream.tile([P, 1536], BF16, name="row_tile", bufs=12)
+            y_raw[h, t] = stream.tile([P, 1536], BF16, name="row_tile", bufs=10)
             nc.sync.dma_start(out=y_raw[h, t][:], in_=y_view[h, t])
 
         lam_view = lam.rearrange("(h q t r) -> h t q r", h=H, t=4, r=8)
         b_cols = keep.tile([P, G, 4], F32, name="b_cols")
-        for h in range(H):
-            nc.scalar.dma_start(out=rows[4 * h : 4 * h + 4, :].rearrange("t (q r) -> t q r", r=8), in_=lam_view[h])
-        nc.scalar.dma_start(out=rows[8:10, :], in_=lam_left.rearrange("(s p) -> s p", p=P))
-        nc.scalar.dma_start(out=right_row[0:1, :], in_=lam_right.rearrange("(o j) -> o j", o=1))
-        nc.scalar.dma_start(out=b_cols[:], in_=b_scale.rearrange("(g p t) o u -> p g (t o u)", p=P, t=4))
-
-        for e in range(4):
-            load_a(0, e)
+        load_a(0, 0)
+        load_a(0, 1)
         xs_view = x_scales.bitcast(I32).rearrange("g q w -> q g w")
         for quad in range(4):
             nc.sync.dma_start(out=xs_raw[32 * quad : 32 * quad + 4, :, :], in_=xs_view[4 * quad : 4 * quad + 4])
-        x_raw = keep.tile([P, G, 512], I32, name="x_raw")
-        nc.sync.dma_start(out=x_raw[:], in_=x_words.bitcast(I32).rearrange("g p w -> p g w"))
+        load_a(0, 2)
+        load_a(0, 3)
+        x_raw = {}
+        x_view = x_words.bitcast(I32)
+        for g in range(G):
+            x_raw[g] = keep.tile([P, 512], I32, name="x_raw_%d" % g)
+            nc.sync.dma_start(out=x_raw[g][:], in_=x_view[g])
+        for h in range(H):
+            nc.sync.dma_start(out=rows[4 * h : 4 * h + 4, :].rearrange("t (q r) -> t q r", r=8), in_=lam_view[h])
+        nc.sync.dma_start(out=b_cols[:], in_=b_scale.rearrange("(g p t) o u -> p g (t o u)", p=P, t=4))
+
         b_raw = keep.tile([P, G, 4096], U8, name="b_raw")
         b_view = b_bytes.rearrange("(g p t) f j -> g p (t f j)", p=P, t=4)
         for g in range(G):
@@ -79,10 +84,13 @@ def tile_two_site_tensor_s11_kernel(tc, a, x_words, x_scales, y, b_bytes, b_scal
         for h in range(H):
             for t in range(4):
                 load_y(h, t)
+            if h == 0:
+                nc.sync.dma_start(out=left_rows[0:2, :], in_=lam_left.rearrange("(s p) -> s p", p=P))
+                nc.sync.dma_start(out=right_row[0:1, :], in_=lam_right.rearrange("(o j) -> o j", o=1))
         for e in range(4):
             load_a(1, e)
 
-        x_codes = keep.tile([P, 4, G, H, 256], U8, name="x_codes", align_bytes=64)
+        x_codes = keep.tile([P, G, 4, H, 256], U8, name="x_codes", align_bytes=64)
         x_plane = keep.tile([P, 4, G, H, 128], U8, name="x_plane", align_bytes=64)
         codes = {}
         planes = {}
@@ -104,14 +112,24 @@ def tile_two_site_tensor_s11_kernel(tc, a, x_words, x_scales, y, b_bytes, b_scal
 
         grouped = {}
 
-        def turn(n, raws, pair, g, engine):
+        sorted_words = {}
+
+        def sort_words(key, raw, engine):
+            sorted_words[key] = stream.tile([P, G, 2, 128], F32, name="sorted", bufs=2)
+            copy_out(engine, sorted_words[key][:], raw[:].bitcast(F32).rearrange("p (g w u) -> p g u w", g=G, u=2))
+
+        def turn(n, pair, g, engine):
+            raws = a_raw if n[0] == "a" else y_raw
             if pair == 0:
                 grouped[n, g] = stream.tile([P, 2048], BF16, name="grouped", bufs=6, align_bytes=64)
-            acc = psum.tile([P, 2, 256], F32, name="turned", bufs=3)
+            acc = psum.tile([P, 2, 256], F32, name="bank", bufs=8)
             for x in range(2):
-                words = raws[2 * pair + x][:].bitcast(F32)
+                key = (int(n[1]), 2 * pair + x)
                 for u in range(2):
-                    src = words[:, 256 * g + u : 256 * (g + 1) : 2]
+                    if (n, key) in sorted_words:
+                        src = sorted_words[n, key][:, g, u, :]
+                    else:
+                        src = raws[key][:].bitcast(F32)[:, 256 * g + u : 256 * (g + 1) : 2]
                     if n[0] == "a":
                         nc.tensor.transpose(acc[:, u, 128 * x : 128 * (x + 1)], src, ident[:])
                     else:
@@ -124,29 +142,46 @@ def tile_two_site_tensor_s11_kernel(tc, a, x_words, x_scales, y, b_bytes, b_scal
                 dst = dst.rearrange("p (t x c u) -> p x t c u", t=4, x=2, u=2)[:, pair]
                 copy_out(engine, dst, acc[:].rearrange("p u (t c) -> p t c u", t=4))
 
-        def quantize(n, c, tile_bf):
-            nc.vector.quantize_mx(out=codes[n][:, c, :].bitcast(FP8X4), scales=planes[n][:, c, :], in_=tile_bf[:])
+        def turn_late(n, pair, engines):
+            accs = [psum.tile([P, 2, 256], F32, name="bank", bufs=8) for g in range(G)]
+            for x in range(2):
+                words = a_raw[int(n[1]), 2 * pair + x][:].bitcast(F32)
+                for g in range(G):
+                    for u in range(2):
+                        nc.tensor.transpose(accs[g][:, u, 128 * x : 128 * (x + 1)], words[:, 256 * g + u : 256 * (g + 1) : 2], ident[:])
+            for g in range(G):
+                if pair == 0:
+                    grouped[n, g] = stream.tile([P, 2048], BF16, name="grouped", bufs=6, align_bytes=64)
+                dst = grouped[n, g][:].bitcast(F32)[:, 512 * pair : 512 * (pair + 1)].rearrange("p (c u) -> p c u", u=2)
+                copy_out(engines[g], dst, accs[g][:].rearrange("p u c -> p c u"))
 
-        def permute_x():
+        def quantize(n, c):
+            nc.vector.quantize_mx(out=codes[n][:, c, :].bitcast(FP8X4), scales=planes[n][:, c, :], in_=grouped[n, c][:])
+
+        def permute_scales():
             nc.vector.tensor_copy(
                 out=x_plane[:].rearrange("p t g h c -> p (t g h c)").bitcast(I32).rearrange("p (t c r) -> p t c r", t=4, r=2),
                 in_=xs_raw[:].rearrange("p g w -> p (g w)").rearrange("p (c t r) -> p t c r", t=4, r=2),
             )
+
+        def permute_words(g):
             nc.vector.tensor_copy(
-                out=x_codes[:].rearrange("p t g h c -> p (t g h c)").bitcast(I32).rearrange("p (t c r) -> p t c r", t=4, r=4),
-                in_=x_raw[:].rearrange("p g w -> p (g w)").rearrange("p (c t r) -> p t c r", t=4, r=4),
+                out=x_codes[:, g].rearrange("p t h c -> p (t h c)").bitcast(I32).rearrange("p (t c r) -> p t c r", t=4, r=4),
+                in_=x_raw[g][:].rearrange("p (c t r) -> p t c r", t=4, r=4),
             )
 
         wide = {}
 
-        def widen(g, t, engine):
-            if t == 0:
+        def widen(g, t, half, engine):
+            if t == 0 and half == 0:
                 wide[g] = stream.tile([P, 4, 1024], BF16, name="wide", bufs=3, align_bytes=64)
-            src = b_raw[:, g, 1024 * t : 1024 * (t + 1)].bitcast(FP8)
+            lo = 512 * half
+            src = b_raw[:, g, 1024 * t + lo : 1024 * t + lo + 512].bitcast(FP8)
+            dst = wide[g][:, t, lo : lo + 512]
             if engine == "S":
-                nc.scalar.activation(out=wide[g][:, t, :], in_=src, func=COPY, scale=b_cols[:, g, t : t + 1])
+                nc.scalar.activation(out=dst, in_=src, func=COPY, scale=b_cols[:, g, t : t + 1])
             else:
-                nc.vector.tensor_scalar(out=wide[g][:, t, :], in0=src, scalar1=b_cols[:, g, t : t + 1], scalar2=None, op0=MULT)
+                nc.vector.tensor_scalar(out=dst, in0=src, scalar1=b_cols[:, g, t : t + 1], scalar2=None, op0=MULT)
 
         inter = {}
 
@@ -168,13 +203,13 @@ def tile_two_site_tensor_s11_kernel(tc, a, x_words, x_scales, y, b_bytes, b_scal
 
         def l_mm(s, h):
             for t in range(4):
-                l_acc[t] = psum.tile([P, 512], F32, name="acc", bufs=5)
+                l_acc[s, h, t] = psum.tile([P, 512], F32, name="bank", bufs=8)
             n = "a%d" % s
             for g in range(G):
                 for t in range(4):
                     nc.tensor.matmul_mx(
-                        out=l_acc[t][:],
-                        lhsT=x_codes[:, t, g, h, :].bitcast(FP4X4),
+                        out=l_acc[s, h, t][:],
+                        lhsT=x_codes[:, g, t, h, :].bitcast(FP4X4),
                         lhsT_scale=x_plane[:, t, g, h, :],
                         rhs=codes[n][:, g, :].bitcast(FP8X4),
                         rhs_scale=planes[n][:, g, :],
@@ -187,9 +222,9 @@ def tile_two_site_tensor_s11_kernel(tc, a, x_words, x_scales, y, b_bytes, b_scal
                 l_wide[s, h] = stream.tile([P, 4, 512], BF16, name="l_wide", bufs=3, align_bytes=64)
             scale = lam_cols[:, 4 * h + t : 4 * h + t + 1]
             if engine == "S":
-                nc.scalar.activation(out=l_wide[s, h][:, t, :], in_=l_acc[t][:], func=COPY, scale=scale)
+                nc.scalar.activation(out=l_wide[s, h][:, t, :], in_=l_acc[s, h, t][:], func=COPY, scale=scale)
             else:
-                nc.vector.tensor_scalar(out=l_wide[s, h][:, t, :], in0=l_acc[t][:], scalar1=scale, scalar2=None, op0=MULT)
+                nc.vector.tensor_scalar(out=l_wide[s, h][:, t, :], in0=l_acc[s, h, t][:], scalar1=scale, scalar2=None, op0=MULT)
 
         def l_inter(s, h):
             interleave(("l", s, h), l_wide[s, h][:])
@@ -200,11 +235,18 @@ def tile_two_site_tensor_s11_kernel(tc, a, x_words, x_scales, y, b_bytes, b_scal
 
         r_group = {}
 
-        def r_mm(h, n, engine):
+        r_acc = {}
+
+        def r_out(h, n, engine):
+            half, m = divmod(n, 4)
+            copy_out(engine, r_group[h, half][:, 128 * m : 128 * (m + 1), :], r_acc[h, n][:].rearrange("p t n -> p n t"))
+
+        def r_mm(h, n):
             half, m = divmod(n, 4)
             if m == 0:
                 r_group[h, half] = stream.tile([P, 512, 4], BF16, name="r_group", bufs=3, align_bytes=64)
-            acc = psum.tile([P, 4, 128], F32, name="acc", bufs=5)
+            acc = psum.tile([P, 4, 128], F32, name="bank", bufs=8)
+            r_acc[h, n] = acc
             yn, bn = "y%d" % h, "b%d" % half
             for t in range(4):
                 for g in range(G):
@@ -217,7 +259,6 @@ def tile_two_site_tensor_s11_kernel(tc, a, x_words, x_scales, y, b_bytes, b_scal
                         start=(g == 0),
                         stop=(g == G - 1),
                     )
-            copy_out(engine, r_group[h, half][:, 128 * m : 128 * (m + 1), :], acc[:].rearrange("p t n -> p n t"))
 
         def r_quant(h, half):
             n = "r%d" % half
@@ -225,8 +266,10 @@ def tile_two_site_tensor_s11_kernel(tc, a, x_words, x_scales, y, b_bytes, b_scal
 
         out_view = out.rearrange("(s p e) n -> s e p n", p=P, e=4)
 
+        t_acc = {}
+
         def theta(s, e, half):
-            acc = psum.tile([P, 512], F32, name="acc", bufs=5)
+            acc = psum.tile([P, 512], F32, name="bank", bufs=8)
             ln, rn = "l%d" % s, "r%d" % half
             for h in range(H):
                 nc.tensor.matmul_mx(
@@ -238,107 +281,135 @@ def tile_two_site_tensor_s11_kernel(tc, a, x_words, x_scales, y, b_bytes, b_scal
                     start=(h == 0),
                     stop=(h == H - 1),
                 )
-            o = stream.tile([P, 512], F32, name="o", bufs=6)
-            nc.vector.scalar_tensor_tensor(out=o[:], in0=acc[:], scalar=lam_cols[:, 8 + s : 9 + s], in1=right[:], op0=MULT, op1=MULT)
+            t_acc[s, e, half] = acc
+
+        def theta_out(s, e, half, engine):
+            acc = t_acc[s, e, half]
+            o = stream.tile([P, 512], F32, name="o", tag="row_tile", bufs=10)
+            if engine == "S":
+                half_done = stream.tile([P, 512], F32, name="half_done", tag="sorted", bufs=2)
+                nc.scalar.activation(out=half_done[:], in_=acc[:], func=COPY, scale=left_cols[:, s : s + 1])
+                nc.gpsimd.tensor_tensor(out=o[:], in0=half_done[:], in1=right[:], op=MULT)
+            else:
+              nc.vector.scalar_tensor_tensor(out=o[:], in0=acc[:], scalar=left_cols[:, s : s + 1], in1=right[:], op0=MULT, op1=MULT)
             nc.sync.dma_start(out=out_view[s, e][:, 512 * half : 512 * (half + 1)], in_=o[:])
 
-        def raw_of(d, i):
-            return [d[i, j] for j in range(4)]
+        turn_late("a0", 0, "VSV")
+        permute_scales()
+        permute_words(0)
+        turn_late("a0", 1, "SVS")
+        quantize("a0", 0)
+        permute_words(1)
+        quantize("a0", 1)
+        permute_words(2)
+        quantize("a0", 2)
 
-        for g in range(G):
-            turn("a0", raw_of(a_raw, 0), 0, g, "VSV"[g])
-        for g in range(G):
-            turn("a0", raw_of(a_raw, 0), 1, g, "SVS"[g])
-        quantize("a0", 0, grouped["a0", 0])
-        permute_x()
-        quantize("a0", 1, grouped["a0", 1])
-        quantize("a0", 2, grouped["a0", 2])
-
-        lam_cols = keep.tile([P, 10], F32, name="lam_cols")
-        lam_ps = psum.tile([P, P], BF16, name="turned", bufs=3)
+        lam_cols = keep.tile([P, 8], F32, name="lam_cols")
+        lam_ps = psum.tile([P, P], BF16, name="bank", bufs=8)
         nc.tensor.transpose(lam_ps[:], rows[:], ident_bf[:])
-        nc.scalar.copy(out=lam_cols[:], in_=lam_ps[:, 0:10])
-        right = keep.tile([P, 512], F32, name="right")
-        right_ps = psum.tile([P, 2, 256], F32, name="acc", bufs=5)
-        for f in range(2):
-            nc.tensor.matmul(right_ps[:, f, :], lhsT=ones[:], rhs=right_row[:], start=True, stop=True)
-        nc.scalar.copy(out=right[:], in_=right_ps[:].rearrange("p f j -> p (f j)"))
+        nc.scalar.copy(out=lam_cols[:], in_=lam_ps[:, 0:8])
 
-        for g in range(G):
-            for t in range(4):
-                widen(g, t, "S" if (g, t) in ((0, 0), (0, 1)) else "V")
         l_mm(0, 0)
-        for t in range(4):
-            l_out(0, 0, t, "S")
         l_mm(0, 1)
         for t in range(4):
-            l_out(0, 1, t, "S")
-
-        for pair in range(2):
-            for g in range(G):
-                turn("y0", raw_of(y_raw, 0), pair, g, "S")
+            widen(0, t, 0, "SSSV"[t])
+        widen(1, 0, 0, "S")
+        widen(1, 1, 0, "V")
+        widen(1, 2, 0, "V")
+        widen(1, 3, 0, "S")
         b_inter(0, 0)
+        for t in range(3):
+            l_out(0, 0, t, "S")
+        l_out(0, 0, 3, "V")
+        for t in range(4):
+            widen(2, t, 0, "VSSV"[t])
         b_inter(1, 0)
         b_quant(0, 0)
+        for t in range(3):
+            l_out(0, 1, t, "S")
+        l_out(0, 1, 3, "V")
         b_inter(2, 0)
         b_quant(1, 0)
-        quantize("y0", 0, grouped["y0", 0])
-        b_quant(2, 0)
-        quantize("y0", 1, grouped["y0", 1])
-        quantize("y0", 2, grouped["y0", 2])
 
-        for pair in range(2):
-            for g in range(G):
-                turn("y1", raw_of(y_raw, 1), pair, g, "S")
+        for i in range(6):
+            turn("y0", i // 3, i % 3, "SSSSSV"[i])
+            if i == 4:
+                b_quant(2, 0)
+        quantize("y0", 0)
+        for t in range(3):
+            widen(0, t, 1, "V")
+        quantize("y0", 1)
+        quantize("y0", 2)
+
+        for i in range(6):
+            turn("y1", i // 3, i % 3, "SSVSSV"[i])
+        widen(0, 3, 1, "V")
+        widen(1, 0, 1, "V")
+
+        for i in range(6):
+            turn("a1", i // 3, i % 3, "SSVSSV"[i])
+            if i in (1, 3, 5):
+                quantize("y1", i // 2)
+            if i in (2, 4):
+                widen(1, i // 2, 1, "S")
+
+        right = keep.tile([P, 512], F32, name="right")
+        right_ps = psum.tile([P, 2, 256], F32, name="bank", bufs=8)
+        for f in range(2):
+            nc.tensor.matmul(right_ps[:, f, :], lhsT=ones[:], rhs=right_row[:], start=True, stop=True)
+        left_cols = keep.tile([P, 2], F32, name="left_cols")
+        left_ps = psum.tile([P, 2], F32, name="bank", bufs=8)
+        nc.tensor.matmul(left_ps[:], lhsT=left_rows[:], rhs=ident_bf[:, 0:2], start=True, stop=True)
+        for n in range(4):
+            r_mm(0, n)
+            r_out(0, n, "SSSS"[n])
+            if n < 3:
+                widen(2, n, 1, "S")
+        widen(1, 3, 1, "V")
+        widen(2, 3, 1, "V")
+        quantize("a1", 0)
         b_inter(0, 1)
-        quantize("y1", 0, grouped["y1", 0])
-        b_quant(0, 1)
-        quantize("y1", 1, grouped["y1", 1])
-        quantize("y1", 2, grouped["y1", 2])
-
-        for pair in range(2):
-            for g in range(G):
-                turn("a1", raw_of(a_raw, 1), pair, g, "S")
-        b_inter(1, 1)
-        quantize("a1", 0, grouped["a1", 0])
-        b_quant(1, 1)
-        quantize("a1", 1, grouped["a1", 1])
-        quantize("a1", 2, grouped["a1", 2])
-
-        for n in range(4):
-            r_mm(0, n, "S")
-        b_inter(2, 1)
+        quantize("a1", 1)
         l_inter(0, 0)
-        b_quant(2, 1)
-        l_quant(0, 0)
-        l_inter(0, 1)
+        quantize("a1", 2)
+        b_inter(1, 1)
         for n in range(4):
-            r_mm(1, n, "S")
-        r_quant(0, 0)
+            r_mm(1, n)
+            r_out(1, n, "SSSS"[n])
+        l_quant(0, 0)
+        b_quant(0, 1)
+        b_inter(2, 1)
+        b_quant(1, 1)
+        l_inter(0, 1)
+        b_quant(2, 1)
         l_quant(0, 1)
+        r_quant(0, 0)
+        nc.scalar.copy(out=right[:], in_=right_ps[:].rearrange("p f j -> p (f j)"))
+        nc.scalar.copy(out=left_cols[:], in_=left_ps[:])
         l_mm(1, 0)
         r_quant(1, 0)
         for t in range(4):
-            l_out(1, 0, t, "SVSV"[t])
+            l_out(1, 0, t, "S")
         l_mm(1, 1)
         l_inter(1, 0)
         for t in range(4):
-            l_out(1, 1, t, "SVSV"[t])
+            l_out(1, 1, t, "S")
         l_quant(1, 0)
         for n in range(4, 8):
-            r_mm(0, n, "S")
+            r_mm(0, n)
+            r_out(0, n, "S")
         l_inter(1, 1)
         l_quant(1, 1)
-        for e in range(4):
+        for e in range(1):
             theta(0, e, 0)
+            theta_out(0, e, 0, "V")
         r_quant(0, 1)
         for n in range(4, 8):
-            r_mm(1, n, "S")
-        for e in range(4):
-            theta(1, e, 0)
-            if e == 0:
+            r_mm(1, n)
+            r_out(1, n, "SSSS"[n-4])
+        rest = [(s, e, 0) for s in range(2) for e in range(4)][1:] + [(s, e, 1) for s in range(2) for e in range(4)]
+        for i, key in enumerate(rest):
+            theta(*key)
+            theta_out(*key, "VVVVVVVVVVVVVVVVV"[i])
+            if i == 1:
                 r_quant(1, 1)
-        for e in range(4):
-            theta(0, e, 1)
-        for e in range(4):
-            theta(1, e, 1)

@@ -35,16 +35,12 @@ def tile_two_site_tensor_s11_kernel(tc, a, x_words, x_scales, y, b_bytes, b_scal
         nc.gpsimd.tensor_copy(out=ident_y[:].rearrange("p t (q r) -> p t q r", r=8), in_=ident[:].rearrange("p (q t r) -> p t q r", q=4, t=4))
         ident_bf = keep.tile([P, P], BF16, name="ident_bf")
         make_identity(nc, ident_bf[:])
-        ones = keep.tile([P, P], BF16, name="ones")
-        nc.gpsimd.memset(ones[:], 1.0)
-        left_rows = keep.tile([P, P], BF16, name="left_rows")
-        right_row = keep.tile([P, 256], BF16, name="right_row")
+        warm = keep.tile([P, 512], BF16, name="warm")
+        nc.gpsimd.memset(warm[:], 0.0)
         xs_raw = keep.tile([P, G, 256], I32, name="xs_raw")
         nc.vector.memset(xs_raw[:], 0)
         rows = keep.tile([P, P], BF16, name="rows")
         nc.vector.memset(rows[:], 0.0)
-        nc.vector.memset(left_rows[:], 0.0)
-        nc.vector.memset(right_row[:], 0.0)
 
         a_raw = {}
         a_view = a.rearrange("(s p) e k -> s e p k", p=P)
@@ -75,6 +71,7 @@ def tile_two_site_tensor_s11_kernel(tc, a, x_words, x_scales, y, b_bytes, b_scal
             nc.sync.dma_start(out=x_raw[g][:], in_=x_view[g])
         for h in range(H):
             nc.sync.dma_start(out=rows[4 * h : 4 * h + 4, :].rearrange("t (q r) -> t q r", r=8), in_=lam_view[h])
+        nc.sync.dma_start(out=rows[8:10, :], in_=lam_left.rearrange("(s p) -> s p", p=P))
         nc.sync.dma_start(out=b_cols[:], in_=b_scale.rearrange("(g p t) o u -> p g (t o u)", p=P, t=4))
 
         b_raw = keep.tile([P, G, 4096], U8, name="b_raw")
@@ -84,11 +81,13 @@ def tile_two_site_tensor_s11_kernel(tc, a, x_words, x_scales, y, b_bytes, b_scal
         for h in range(H):
             for t in range(4):
                 load_y(h, t)
-            if h == 0:
-                nc.sync.dma_start(out=left_rows[0:2, :], in_=lam_left.rearrange("(s p) -> s p", p=P))
-                nc.sync.dma_start(out=right_row[0:1, :], in_=lam_right.rearrange("(o j) -> o j", o=1))
         for e in range(4):
             load_a(1, e)
+        right_bf = keep.tile([P, 256], BF16, name="right_bf")
+        nc.sync.dma_start(out=right_bf[:], in_=lam_right.partition_broadcast(P))
+        right = keep.tile([P, 2, 256], F32, name="right")
+        for f in range(2):
+            nc.gpsimd.tensor_copy(out=right[:, f, :], in_=right_bf[:])
 
         x_codes = keep.tile([P, G, 4, H, 256], U8, name="x_codes", align_bytes=64)
         x_plane = keep.tile([P, 4, G, H, 128], U8, name="x_plane", align_bytes=64)
@@ -155,8 +154,8 @@ def tile_two_site_tensor_s11_kernel(tc, a, x_words, x_scales, y, b_bytes, b_scal
                 dst = grouped[n, g][:].bitcast(F32)[:, 512 * pair : 512 * (pair + 1)].rearrange("p (c u) -> p c u", u=2)
                 copy_out(engines[g], dst, accs[g][:].rearrange("p u c -> p c u"))
 
-        def quantize(n, c):
-            nc.vector.quantize_mx(out=codes[n][:, c, :].bitcast(FP8X4), scales=planes[n][:, c, :], in_=grouped[n, c][:])
+        def quantize(n, c, lo=0, hi=512):
+            nc.vector.quantize_mx(out=codes[n][:, c, lo:hi].bitcast(FP8X4), scales=planes[n][:, c, lo:hi], in_=grouped[n, c][:, 4 * lo : 4 * hi])
 
         def permute_scales():
             nc.vector.tensor_copy(
@@ -187,7 +186,7 @@ def tile_two_site_tensor_s11_kernel(tc, a, x_words, x_scales, y, b_bytes, b_scal
 
         def interleave(key, src):
             inter[key] = stream.tile([P, 512, 4], BF16, name="inter", bufs=4, align_bytes=64)
-            nc.vector.tensor_copy(out=inter[key][:], in_=src.rearrange("p t n -> p n t"))
+            nc.vector.tensor_copy(out=inter[key][:].rearrange("p (c i) t -> p c t i", i=4), in_=src.rearrange("p t (c i) -> p c t i", i=4))
 
         def inter_flat(key):
             return inter[key][:].rearrange("p n t -> p (n t)")
@@ -283,51 +282,51 @@ def tile_two_site_tensor_s11_kernel(tc, a, x_words, x_scales, y, b_bytes, b_scal
                 )
             t_acc[s, e, half] = acc
 
-        def theta_out(s, e, half, engine):
+        def theta_out(s, e, half, parts=1):
             acc = t_acc[s, e, half]
-            o = stream.tile([P, 512], F32, name="o", tag="row_tile", bufs=10)
-            if engine == "S":
-                half_done = stream.tile([P, 512], F32, name="half_done", tag="sorted", bufs=2)
-                nc.scalar.activation(out=half_done[:], in_=acc[:], func=COPY, scale=left_cols[:, s : s + 1])
-                nc.gpsimd.tensor_tensor(out=o[:], in0=half_done[:], in1=right[:], op=MULT)
-            else:
-              nc.vector.scalar_tensor_tensor(out=o[:], in0=acc[:], scalar=left_cols[:, s : s + 1], in1=right[:], op0=MULT, op1=MULT)
-            nc.sync.dma_start(out=out_view[s, e][:, 512 * half : 512 * (half + 1)], in_=o[:])
+            width = 512 // parts
+            for i in range(parts):
+                lo = width * i
+                o = stream.tile([P, 512], F32, name="o", tag="row_tile", bufs=10)
+                nc.vector.scalar_tensor_tensor(out=o[:, 0:width], in0=acc[:, lo : lo + width], scalar=lam_cols[:, 8 + s : 9 + s], in1=right[:].rearrange("p f j -> p (f j)")[:, lo : lo + width], op0=MULT, op1=MULT)
+                nc.sync.dma_start(out=out_view[s, e][:, 512 * half + lo : 512 * half + lo + width], in_=o[:, 0:width])
 
         turn_late("a0", 0, "VSV")
         permute_scales()
-        permute_words(0)
+        for g in range(G):
+            quantize("a0", g, 0, 256)
         turn_late("a0", 1, "SVS")
-        quantize("a0", 0)
+        permute_words(0)
+        quantize("a0", 0, 256, 512)
         permute_words(1)
-        quantize("a0", 1)
+        quantize("a0", 1, 256, 512)
         permute_words(2)
-        quantize("a0", 2)
+        quantize("a0", 2, 256, 512)
 
-        lam_cols = keep.tile([P, 8], F32, name="lam_cols")
+        warm_ps = psum.tile([P, 512], F32, name="bank", bufs=8)
+        for i in range(3):
+            nc.tensor.matmul(warm_ps[:], lhsT=ident_bf[:], rhs=warm[:], start=True, stop=True)
+
+        lam_cols = keep.tile([P, 10], F32, name="lam_cols")
         lam_ps = psum.tile([P, P], BF16, name="bank", bufs=8)
         nc.tensor.transpose(lam_ps[:], rows[:], ident_bf[:])
-        nc.scalar.copy(out=lam_cols[:], in_=lam_ps[:, 0:8])
+        nc.scalar.copy(out=lam_cols[:], in_=lam_ps[:, 0:10])
 
         l_mm(0, 0)
         l_mm(0, 1)
         for t in range(4):
             widen(0, t, 0, "SSSV"[t])
-        widen(1, 0, 0, "S")
-        widen(1, 1, 0, "V")
-        widen(1, 2, 0, "V")
-        widen(1, 3, 0, "S")
+        for t in range(4):
+            widen(1, t, 0, "SVVS"[t])
         b_inter(0, 0)
-        for t in range(3):
-            l_out(0, 0, t, "S")
-        l_out(0, 0, 3, "V")
+        for t in range(4):
+            l_out(0, 0, t, "SSSV"[t])
         for t in range(4):
             widen(2, t, 0, "VSSV"[t])
         b_inter(1, 0)
         b_quant(0, 0)
-        for t in range(3):
-            l_out(0, 1, t, "S")
-        l_out(0, 1, 3, "V")
+        for t in range(4):
+            l_out(0, 1, t, "SSSV"[t])
         b_inter(2, 0)
         b_quant(1, 0)
 
@@ -346,6 +345,9 @@ def tile_two_site_tensor_s11_kernel(tc, a, x_words, x_scales, y, b_bytes, b_scal
         widen(0, 3, 1, "V")
         widen(1, 0, 1, "V")
 
+        for e in range(4):
+            if "----"[e] != "-":
+                sort_words(("a1", (1, e)), a_raw[1, e], "----"[e])
         for i in range(6):
             turn("a1", i // 3, i % 3, "SSVSSV"[i])
             if i in (1, 3, 5):
@@ -353,18 +355,11 @@ def tile_two_site_tensor_s11_kernel(tc, a, x_words, x_scales, y, b_bytes, b_scal
             if i in (2, 4):
                 widen(1, i // 2, 1, "S")
 
-        right = keep.tile([P, 512], F32, name="right")
-        right_ps = psum.tile([P, 2, 256], F32, name="bank", bufs=8)
-        for f in range(2):
-            nc.tensor.matmul(right_ps[:, f, :], lhsT=ones[:], rhs=right_row[:], start=True, stop=True)
-        left_cols = keep.tile([P, 2], F32, name="left_cols")
-        left_ps = psum.tile([P, 2], F32, name="bank", bufs=8)
-        nc.tensor.matmul(left_ps[:], lhsT=left_rows[:], rhs=ident_bf[:, 0:2], start=True, stop=True)
         for n in range(4):
             r_mm(0, n)
-            r_out(0, n, "SSSS"[n])
+            r_out(0, n, "S")
             if n < 3:
-                widen(2, n, 1, "S")
+                widen(2, n, 1, "SSS"[n])
         widen(1, 3, 1, "V")
         widen(2, 3, 1, "V")
         quantize("a1", 0)
@@ -375,7 +370,7 @@ def tile_two_site_tensor_s11_kernel(tc, a, x_words, x_scales, y, b_bytes, b_scal
         b_inter(1, 1)
         for n in range(4):
             r_mm(1, n)
-            r_out(1, n, "SSSS"[n])
+            r_out(1, n, "S")
         l_quant(0, 0)
         b_quant(0, 1)
         b_inter(2, 1)
@@ -384,8 +379,6 @@ def tile_two_site_tensor_s11_kernel(tc, a, x_words, x_scales, y, b_bytes, b_scal
         b_quant(2, 1)
         l_quant(0, 1)
         r_quant(0, 0)
-        nc.scalar.copy(out=right[:], in_=right_ps[:].rearrange("p f j -> p (f j)"))
-        nc.scalar.copy(out=left_cols[:], in_=left_ps[:])
         l_mm(1, 0)
         r_quant(1, 0)
         for t in range(4):
@@ -402,14 +395,17 @@ def tile_two_site_tensor_s11_kernel(tc, a, x_words, x_scales, y, b_bytes, b_scal
         l_quant(1, 1)
         for e in range(1):
             theta(0, e, 0)
-            theta_out(0, e, 0, "V")
+            theta_out(0, e, 0)
         r_quant(0, 1)
         for n in range(4, 8):
             r_mm(1, n)
-            r_out(1, n, "SSSS"[n-4])
+            r_out(1, n, "S")
+            if n - 4 < 0:
+                theta(0, n - 4 + 1, 0)
+                theta_out(0, n - 4 + 1, 0)
         rest = [(s, e, 0) for s in range(2) for e in range(4)][1:] + [(s, e, 1) for s in range(2) for e in range(4)]
         for i, key in enumerate(rest):
             theta(*key)
-            theta_out(*key, "VVVVVVVVVVVVVVVVV"[i])
+            theta_out(*key, parts=(2 if i == len(rest) - 1 else 1))
             if i == 1:
                 r_quant(1, 1)

@@ -113,26 +113,30 @@ def tile_two_site_tensor_s11_kernel(tc, a, x_words, x_scales, y, b_bytes, b_scal
 
         sorted_words = {}
 
-        def sort_words(key, raw, engine):
-            sorted_words[key] = stream.tile([P, G, 2, 128], F32, name="sorted", bufs=2)
-            copy_out(engine, sorted_words[key][:], raw[:].bitcast(F32).rearrange("p (g w u) -> p g u w", g=G, u=2))
+        def sort_words(n, e, engine):
+            raw = (a_raw if n[0] == "a" else y_raw)[int(n[1]), e]
+            sorted_words[n, e] = stream.tile([P, G, 2, 128], F32, name="sorted", bufs=4)
+            copy_out(engine, sorted_words[n, e][:], raw[:].bitcast(F32).rearrange("p (g w u) -> p g u w", g=G, u=2))
 
-        def turn(n, pair, g, engine):
-            raws = a_raw if n[0] == "a" else y_raw
-            if pair == 0:
+        turned = {}
+
+        def transpose_words(acc, n, pair, x, g):
+            e = 2 * pair + x
+            raw = (a_raw if n[0] == "a" else y_raw)[int(n[1]), e]
+            for u in range(2):
+                if (n, e) in sorted_words:
+                    src = sorted_words[n, e][:, g, u, :]
+                else:
+                    src = raw[:].bitcast(F32)[:, 256 * g + u : 256 * (g + 1) : 2]
+                if n[0] == "a":
+                    nc.tensor.transpose(acc[:, u, 128 * x : 128 * (x + 1)], src, ident[:])
+                else:
+                    nc.tensor.transpose(acc[:, u, :].rearrange("p (t x c) -> p x t c", t=4, x=2)[:, x], src, ident_y[:].rearrange("p t c -> p (t c)"))
+
+        def empty(n, pair, g, engine):
+            if (n, g) not in grouped:
                 grouped[n, g] = stream.tile([P, 2048], BF16, name="grouped", bufs=6, align_bytes=64)
-            acc = psum.tile([P, 2, 256], F32, name="bank", bufs=8)
-            for x in range(2):
-                key = (int(n[1]), 2 * pair + x)
-                for u in range(2):
-                    if (n, key) in sorted_words:
-                        src = sorted_words[n, key][:, g, u, :]
-                    else:
-                        src = raws[key][:].bitcast(F32)[:, 256 * g + u : 256 * (g + 1) : 2]
-                    if n[0] == "a":
-                        nc.tensor.transpose(acc[:, u, 128 * x : 128 * (x + 1)], src, ident[:])
-                    else:
-                        nc.tensor.transpose(acc[:, u, :].rearrange("p (t x c) -> p x t c", t=4, x=2)[:, x], src, ident_y[:].rearrange("p t c -> p (t c)"))
+            acc = turned[n, pair, g]
             dst = grouped[n, g][:].bitcast(F32)
             if n[0] == "a":
                 dst = dst[:, 512 * pair : 512 * (pair + 1)].rearrange("p (c u) -> p c u", u=2)
@@ -141,18 +145,33 @@ def tile_two_site_tensor_s11_kernel(tc, a, x_words, x_scales, y, b_bytes, b_scal
                 dst = dst.rearrange("p (t x c u) -> p x t c u", t=4, x=2, u=2)[:, pair]
                 copy_out(engine, dst, acc[:].rearrange("p u (t c) -> p t c u", t=4))
 
-        def turn_late(n, pair, engines):
-            accs = [psum.tile([P, 2, 256], F32, name="bank", bufs=8) for g in range(G)]
+        def turn(n, pair, g):
+            acc = psum.tile([P, 2, 256], F32, name="bank", bufs=8)
+            turned[n, pair, g] = acc
             for x in range(2):
-                words = a_raw[int(n[1]), 2 * pair + x][:].bitcast(F32)
-                for g in range(G):
-                    for u in range(2):
-                        nc.tensor.transpose(accs[g][:, u, 128 * x : 128 * (x + 1)], words[:, 256 * g + u : 256 * (g + 1) : 2], ident[:])
+                transpose_words(acc, n, pair, x, g)
+
+        def turn_tile(n, pair, x):
             for g in range(G):
-                if pair == 0:
-                    grouped[n, g] = stream.tile([P, 2048], BF16, name="grouped", bufs=6, align_bytes=64)
-                dst = grouped[n, g][:].bitcast(F32)[:, 512 * pair : 512 * (pair + 1)].rearrange("p (c u) -> p c u", u=2)
-                copy_out(engines[g], dst, accs[g][:].rearrange("p u c -> p c u"))
+                if x == 0:
+                    turned[n, pair, g] = psum.tile([P, 2, 256], F32, name="bank", bufs=8)
+            for g in range(G):
+                transpose_words(turned[n, pair, g], n, pair, x, g)
+
+        def warm_up():
+            warm_ps = psum.tile([P, 512], F32, name="bank", bufs=8)
+            for i in range(3):
+                nc.tensor.matmul(warm_ps[:], lhsT=ident_bf[:], rhs=warm[:], start=True, stop=True)
+
+        lam_cols = keep.tile([P, 10], F32, name="lam_cols")
+        lam_ps = {}
+
+        def lam_turn():
+            lam_ps[0] = psum.tile([P, P], BF16, name="bank", bufs=8)
+            nc.tensor.transpose(lam_ps[0][:], rows[:], ident_bf[:])
+
+        def lam_out():
+            nc.scalar.copy(out=lam_cols[:], in_=lam_ps[0][:, 0:10])
 
         def quantize(n, c, lo=0, hi=512):
             nc.vector.quantize_mx(out=codes[n][:, c, lo:hi].bitcast(FP8X4), scales=planes[n][:, c, lo:hi], in_=grouped[n, c][:, 4 * lo : 4 * hi])
@@ -169,11 +188,9 @@ def tile_two_site_tensor_s11_kernel(tc, a, x_words, x_scales, y, b_bytes, b_scal
                 in_=x_raw[g][:].rearrange("p (c t r) -> p t c r", t=4, r=4),
             )
 
-        wide = {}
+        wide = [keep.tile([P, 4, 1024], BF16, name="wide_%d" % g, align_bytes=64) for g in range(G)]
 
         def widen(g, t, half, engine):
-            if t == 0 and half == 0:
-                wide[g] = stream.tile([P, 4, 1024], BF16, name="wide", bufs=3, align_bytes=64)
             lo = 512 * half
             src = b_raw[:, g, 1024 * t + lo : 1024 * t + lo + 512].bitcast(FP8)
             dst = wide[g][:, t, lo : lo + 512]
@@ -217,7 +234,7 @@ def tile_two_site_tensor_s11_kernel(tc, a, x_words, x_scales, y, b_bytes, b_scal
                     )
 
         def l_out(s, h, t, engine):
-            if t == 0:
+            if (s, h) not in l_wide:
                 l_wide[s, h] = stream.tile([P, 4, 512], BF16, name="l_wide", bufs=3, align_bytes=64)
             scale = lam_cols[:, 4 * h + t : 4 * h + t + 1]
             if engine == "S":
@@ -236,28 +253,29 @@ def tile_two_site_tensor_s11_kernel(tc, a, x_words, x_scales, y, b_bytes, b_scal
 
         r_acc = {}
 
-        def r_out(h, n, engine):
-            half, m = divmod(n, 4)
-            copy_out(engine, r_group[h, half][:, 128 * m : 128 * (m + 1), :], r_acc[h, n][:].rearrange("p t n -> p n t"))
-
-        def r_mm(h, n):
-            half, m = divmod(n, 4)
-            if m == 0:
-                r_group[h, half] = stream.tile([P, 512, 4], BF16, name="r_group", bufs=3, align_bytes=64)
-            acc = psum.tile([P, 4, 128], F32, name="bank", bufs=8)
-            r_acc[h, n] = acc
+        def r_mm(h, m, b):
+            acc = psum.tile([P, 2, 256], F32, name="bank", bufs=8)
+            r_acc[h, m, b] = acc
+            half, lo = m // 2, 256 * (m % 2)
             yn, bn = "y%d" % h, "b%d" % half
-            for t in range(4):
+            for i in range(2):
+                t = 2 * b + i
                 for g in range(G):
                     nc.tensor.matmul_mx(
-                        out=acc[:, t, :],
+                        out=acc[:, i, :],
                         lhsT=codes[yn][:, g, 128 * t : 128 * (t + 1)].bitcast(FP8X4),
                         lhsT_scale=planes[yn][:, g, 128 * t : 128 * (t + 1)],
-                        rhs=codes[bn][:, g, 128 * m : 128 * (m + 1)].bitcast(FP8X4),
-                        rhs_scale=planes[bn][:, g, 128 * m : 128 * (m + 1)],
+                        rhs=codes[bn][:, g, lo : lo + 256].bitcast(FP8X4),
+                        rhs_scale=planes[bn][:, g, lo : lo + 256],
                         start=(g == 0),
                         stop=(g == G - 1),
                     )
+
+        def r_out(h, m, b, engine):
+            half, lo = m // 2, 256 * (m % 2)
+            if (h, half) not in r_group:
+                r_group[h, half] = stream.tile([P, 512, 4], BF16, name="r_group", bufs=3, align_bytes=64)
+            copy_out(engine, r_group[h, half][:, lo : lo + 256, 2 * b : 2 * b + 2], r_acc[h, m, b][:].rearrange("p t n -> p n t"))
 
         def r_quant(h, half):
             n = "r%d" % half
@@ -291,121 +309,203 @@ def tile_two_site_tensor_s11_kernel(tc, a, x_words, x_scales, y, b_bytes, b_scal
                 nc.vector.scalar_tensor_tensor(out=o[:, 0:width], in0=acc[:, lo : lo + width], scalar=lam_cols[:, 8 + s : 9 + s], in1=right[:].rearrange("p f j -> p (f j)")[:, lo : lo + width], op0=MULT, op1=MULT)
                 nc.sync.dma_start(out=out_view[s, e][:, 512 * half + lo : 512 * half + lo + width], in_=o[:, 0:width])
 
-        turn_late("a0", 0, "VSV")
+        turn_tile("a0", 0, 0)
+        turn_tile("a0", 0, 1)
+        turn_tile("a0", 1, 0)
+        turn_tile("a0", 1, 1)
+        empty("a0", 0, 1, "S")
         permute_scales()
-        for g in range(G):
-            quantize("a0", g, 0, 256)
-        turn_late("a0", 1, "SVS")
+        empty("a0", 1, 0, "S")
+        empty("a0", 1, 1, "S")
+        empty("a0", 0, 2, "S")
+        empty("a0", 0, 0, "V")
+        quantize("a0", 0, 0, 256)
+        warm_up()
+        widen(0, 0, 1, "S")
+        quantize("a0", 1, 0, 256)
+        widen(0, 1, 0, "S")
         permute_words(0)
+        empty("a0", 1, 2, "V")
         quantize("a0", 0, 256, 512)
-        permute_words(1)
+        lam_turn()
+        lam_out()
         quantize("a0", 1, 256, 512)
-        permute_words(2)
+        permute_words(1)
         quantize("a0", 2, 256, 512)
-
-        warm_ps = psum.tile([P, 512], F32, name="bank", bufs=8)
-        for i in range(3):
-            nc.tensor.matmul(warm_ps[:], lhsT=ident_bf[:], rhs=warm[:], start=True, stop=True)
-
-        lam_cols = keep.tile([P, 10], F32, name="lam_cols")
-        lam_ps = psum.tile([P, P], BF16, name="bank", bufs=8)
-        nc.tensor.transpose(lam_ps[:], rows[:], ident_bf[:])
-        nc.scalar.copy(out=lam_cols[:], in_=lam_ps[:, 0:10])
-
+        quantize("a0", 2, 0, 256)
+        permute_words(2)
+        widen(0, 2, 0, "V")
+        widen(0, 0, 0, "V")
         l_mm(0, 0)
         l_mm(0, 1)
-        for t in range(4):
-            widen(0, t, 0, "SSSV"[t])
-        for t in range(4):
-            widen(1, t, 0, "SVVS"[t])
-        b_inter(0, 0)
-        for t in range(4):
-            l_out(0, 0, t, "SSSV"[t])
-        for t in range(4):
-            widen(2, t, 0, "VSSV"[t])
-        b_inter(1, 0)
-        b_quant(0, 0)
-        for t in range(4):
-            l_out(0, 1, t, "SSSV"[t])
-        b_inter(2, 0)
-        b_quant(1, 0)
-
-        for i in range(6):
-            turn("y0", i // 3, i % 3, "SSSSSV"[i])
-            if i == 4:
-                b_quant(2, 0)
-        quantize("y0", 0)
-        for t in range(3):
-            widen(0, t, 1, "V")
-        quantize("y0", 1)
-        quantize("y0", 2)
-
-        for i in range(6):
-            turn("y1", i // 3, i % 3, "SSVSSV"[i])
+        l_out(0, 0, 1, "S")
+        widen(1, 3, 0, "V")
+        l_out(0, 0, 2, "S")
+        widen(2, 2, 0, "S")
+        widen(1, 0, 0, "V")
+        widen(2, 3, 0, "S")
+        widen(1, 2, 0, "V")
+        l_out(0, 0, 3, "S")
         widen(0, 3, 1, "V")
-        widen(1, 0, 1, "V")
-
-        for e in range(4):
-            if "----"[e] != "-":
-                sort_words(("a1", (1, e)), a_raw[1, e], "----"[e])
-        for i in range(6):
-            turn("a1", i // 3, i % 3, "SSVSSV"[i])
-            if i in (1, 3, 5):
-                quantize("y1", i // 2)
-            if i in (2, 4):
-                widen(1, i // 2, 1, "S")
-
-        for n in range(4):
-            r_mm(0, n)
-            r_out(0, n, "S")
-            if n < 3:
-                widen(2, n, 1, "SSS"[n])
-        widen(1, 3, 1, "V")
+        widen(1, 2, 1, "V")
+        widen(1, 1, 0, "V")
+        l_out(0, 0, 0, "V")
+        turn("y0", 0, 2)
+        widen(2, 0, 0, "V")
+        turn("y0", 1, 2)
+        widen(2, 1, 0, "S")
+        widen(0, 1, 1, "V")
+        l_out(0, 1, 0, "S")
+        l_out(0, 1, 2, "S")
+        l_out(0, 1, 1, "S")
+        turn("y0", 0, 1)
         widen(2, 3, 1, "V")
+        turn("y0", 1, 0)
+        l_out(0, 1, 3, "S")
+        widen(0, 3, 0, "S")
+        turn("y1", 0, 1)
+        b_inter(1, 0)
+        turn("y0", 0, 0)
+        turn("y0", 1, 1)
+        empty("y0", 1, 0, "S")
+        empty("y0", 0, 2, "S")
+        turn("y1", 0, 2)
+        b_inter(2, 0)
+        empty("y0", 1, 2, "S")
+        empty("y0", 0, 1, "V")
+        empty("y0", 1, 1, "S")
+        b_quant(2, 0)
+        empty("y1", 0, 1, "V")
+        turn("y1", 1, 2)
+        b_inter(0, 0)
+        empty("y0", 0, 0, "S")
+        turn("y1", 1, 1)
+        turn("a1", 0, 2)
+        turn("y1", 0, 0)
+        quantize("y0", 2)
+        empty("y1", 1, 2, "V")
+        empty("y1", 0, 2, "S")
+        widen(1, 3, 1, "V")
+        b_quant(1, 0)
+        turn("a1", 0, 0)
+        widen(2, 0, 1, "S")
+        b_quant(0, 0)
+        widen(2, 2, 1, "S")
+        turn("a1", 0, 1)
+        turn("a1", 1, 2)
+        empty("y1", 1, 1, "S")
+        widen(0, 2, 1, "S")
+        quantize("y0", 0)
+        turn("a1", 1, 0)
+        turn("a1", 1, 1)
+        quantize("y0", 1)
+        empty("a1", 0, 2, "S")
+        empty("y1", 0, 0, "V")
+        empty("a1", 0, 0, "V")
+        quantize("y1", 1)
+        empty("a1", 1, 0, "S")
         quantize("a1", 0)
+        empty("a1", 1, 1, "S")
+        turn("y1", 1, 0)
+        empty("a1", 1, 2, "S")
+        empty("a1", 0, 1, "S")
         b_inter(0, 1)
         quantize("a1", 1)
-        l_inter(0, 0)
+        empty("y1", 1, 0, "S")
+        r_mm(0, 1, 0)
+        r_mm(0, 0, 0)
+        r_out(0, 1, 0, "S")
+        r_out(0, 0, 0, "S")
+        r_mm(0, 1, 1)
+        widen(1, 1, 1, "S")
         quantize("a1", 2)
-        b_inter(1, 1)
-        for n in range(4):
-            r_mm(1, n)
-            r_out(1, n, "S")
-        l_quant(0, 0)
+        l_inter(0, 0)
         b_quant(0, 1)
-        b_inter(2, 1)
-        b_quant(1, 1)
-        l_inter(0, 1)
-        b_quant(2, 1)
-        l_quant(0, 1)
-        r_quant(0, 0)
+        quantize("y1", 0)
+        r_out(0, 1, 1, "S")
+        r_mm(0, 0, 1)
         l_mm(1, 0)
-        r_quant(1, 0)
-        for t in range(4):
-            l_out(1, 0, t, "S")
+        widen(2, 1, 1, "S")
+        r_out(0, 0, 1, "S")
+        b_inter(2, 1)
         l_mm(1, 1)
+        l_out(1, 0, 0, "V")
+        l_out(1, 0, 1, "S")
+        quantize("y1", 2)
+        r_quant(0, 0)
+        widen(1, 0, 1, "S")
+        r_mm(1, 1, 1)
+        b_inter(1, 1)
+        l_out(1, 0, 2, "S")
+        l_out(1, 0, 3, "S")
+        r_mm(1, 0, 0)
+        b_quant(2, 1)
+        b_quant(1, 1)
+        r_mm(1, 0, 1)
+        l_out(1, 1, 2, "S")
+        l_quant(0, 0)
+        r_mm(1, 3, 1)
+        l_out(1, 1, 0, "S")
         l_inter(1, 0)
-        for t in range(4):
-            l_out(1, 1, t, "S")
-        l_quant(1, 0)
-        for n in range(4, 8):
-            r_mm(0, n)
-            r_out(0, n, "S")
+        l_inter(0, 1)
+        r_mm(1, 1, 0)
+        l_out(1, 1, 1, "S")
+        r_mm(1, 2, 0)
+        l_out(1, 1, 3, "S")
+        r_mm(0, 3, 0)
+        r_out(1, 0, 0, "S")
+        r_mm(1, 3, 0)
+        r_out(1, 0, 1, "S")
+        r_out(1, 3, 1, "S")
+        r_out(1, 1, 1, "S")
         l_inter(1, 1)
+        r_mm(1, 2, 1)
+        r_out(1, 1, 0, "S")
+        l_quant(1, 0)
+        r_mm(0, 2, 1)
+        r_quant(1, 0)
+        r_out(1, 2, 0, "S")
+        l_quant(0, 1)
         l_quant(1, 1)
-        for e in range(1):
-            theta(0, e, 0)
-            theta_out(0, e, 0)
+        r_out(1, 3, 0, "S")
+        r_mm(0, 3, 1)
+        theta(0, 2, 0)
+        r_out(0, 3, 0, "S")
+        theta_out(0, 2, 0)
+        theta(0, 3, 0)
+        r_out(1, 2, 1, "S")
+        theta(1, 2, 0)
+        theta(1, 1, 0)
+        r_out(0, 2, 1, "S")
+        r_mm(0, 2, 0)
+        theta_out(0, 3, 0)
+        r_out(0, 3, 1, "S")
+        theta_out(1, 2, 0)
+        r_out(0, 2, 0, "S")
+        theta(0, 1, 0)
+        r_quant(1, 1)
+        theta_out(1, 1, 0)
+        theta(1, 3, 0)
+        theta_out(0, 1, 0)
         r_quant(0, 1)
-        for n in range(4, 8):
-            r_mm(1, n)
-            r_out(1, n, "S")
-            if n - 4 < 0:
-                theta(0, n - 4 + 1, 0)
-                theta_out(0, n - 4 + 1, 0)
-        rest = [(s, e, 0) for s in range(2) for e in range(4)][1:] + [(s, e, 1) for s in range(2) for e in range(4)]
-        for i, key in enumerate(rest):
-            theta(*key)
-            theta_out(*key, parts=(2 if i == len(rest) - 1 else 1))
-            if i == 1:
-                r_quant(1, 1)
+        theta(1, 0, 0)
+        theta(0, 0, 0)
+        theta(1, 2, 1)
+        theta_out(1, 3, 0)
+        theta_out(0, 0, 0)
+        theta(0, 3, 1)
+        theta(0, 2, 1)
+        theta_out(1, 0, 0)
+        theta(1, 1, 1)
+        theta(0, 0, 1)
+        theta(1, 0, 1)
+        theta_out(0, 3, 1)
+        theta_out(1, 2, 1)
+        theta_out(1, 1, 1)
+        theta_out(0, 0, 1)
+        theta(0, 1, 1)
+        theta_out(1, 0, 1)
+        theta(1, 3, 1)
+        theta_out(0, 2, 1)
+        theta_out(1, 3, 1)
+        theta_out(0, 1, 1, parts=2)

@@ -17,495 +17,382 @@ COPY = mybir.ActivationFunctionType.Copy
 MULT = mybir.AluOpType.mult
 
 P = 128
+OLD = 1536
 G = 3
 H = 2
+T = 4
+E = 4
+HALF = 512
+BANKS = 8
 
 
-def tile_two_site_tensor_s11_kernel(tc, a, x_words, x_scales, y, b_bytes, b_scale, lam, lam_left, lam_right, out):
+def tile_two_site_tensor_s11_kernel(
+    tc, a, x_words, x_scales, y, b_bytes, b_scale, lam, lam_left, lam_right, out
+):
     nc = tc.nc
     with ExitStack() as ctx:
         keep = ctx.enter_context(tc.tile_pool(name="keep", bufs=1))
         stream = ctx.enter_context(tc.tile_pool(name="stream", bufs=2))
-        psum = ctx.enter_context(tc.psum_pool(name="psum", bufs=2))
+        psum = ctx.enter_context(tc.psum_pool(name="psum", bufs=BANKS))
         ctx.enter_context(tc.manual_schedule())
 
-        ident = keep.tile([P, P], F32, name="ident")
-        make_identity(nc, ident[:])
-        ident_y = keep.tile([P, 4, 32], F32, name="ident_y")
-        nc.gpsimd.tensor_copy(out=ident_y[:].rearrange("p t (q r) -> p t q r", r=8), in_=ident[:].rearrange("p (q t r) -> p t q r", q=4, t=4))
-        ident_bf = keep.tile([P, P], BF16, name="ident_bf")
-        make_identity(nc, ident_bf[:])
-        warm = keep.tile([P, 512], BF16, name="warm")
-        nc.gpsimd.memset(warm[:], 0.0)
-        xs_raw = keep.tile([P, G, 256], I32, name="xs_raw")
-        nc.vector.memset(xs_raw[:], 0)
-        rows = keep.tile([P, P], BF16, name="rows")
-        nc.vector.memset(rows[:], 0.0)
+        identity = keep.tile([P, P], F32, name="identity")
+        make_identity(nc, identity[:])
+        by_code = keep.tile([P, P], F32, name="by_code")
+        nc.gpsimd.tensor_copy(
+            out=by_code[:].rearrange("p (t q r) -> p t q r", t=T, r=8),
+            in_=identity[:].rearrange("p (q t r) -> p t q r", t=T, r=8),
+        )
+        identity_bf = keep.tile([P, P], BF16, name="identity_bf")
+        make_identity(nc, identity_bf[:])
+        zeros = keep.tile([P, HALF], BF16, name="zeros")
+        nc.gpsimd.memset(zeros[:], 0.0)
 
-        a_raw = {}
+        x_scale_raw = keep.tile([P, G, 256], I32, name="x_scale_raw")
+        nc.vector.memset(x_scale_raw[:], 0)
+        schmidt_rows = keep.tile([P, P], BF16, name="schmidt_rows")
+        nc.vector.memset(schmidt_rows[:], 0.0)
+
         a_view = a.rearrange("(s p) e k -> s e p k", p=P)
-        y_raw = {}
         y_view = y.rearrange("(h j p) k -> h j p k", h=H, p=P)
+        row_tiles = {}
 
-        def load_a(s, e):
-            a_raw[s, e] = stream.tile([P, 1536], BF16, name="row_tile", bufs=10)
-            nc.sync.dma_start(out=a_raw[s, e][:], in_=a_view[s, e])
+        def load_rows(operand, i):
+            view = a_view if operand[0] == "a" else y_view
+            row_tiles[operand, i] = stream.tile([P, OLD], BF16, name="row_tile", bufs=10)
+            nc.sync.dma_start(out=row_tiles[operand, i][:], in_=view[int(operand[1]), i])
 
-        def load_y(h, t):
-            y_raw[h, t] = stream.tile([P, 1536], BF16, name="row_tile", bufs=10)
-            nc.sync.dma_start(out=y_raw[h, t][:], in_=y_view[h, t])
-
-        lam_view = lam.rearrange("(h q t r) -> h t q r", h=H, t=4, r=8)
-        b_cols = keep.tile([P, G, 4], F32, name="b_cols")
-        load_a(0, 0)
-        load_a(0, 1)
-        xs_view = x_scales.bitcast(I32).rearrange("g q w -> q g w")
-        for quad in range(4):
-            nc.sync.dma_start(out=xs_raw[32 * quad : 32 * quad + 4, :, :], in_=xs_view[4 * quad : 4 * quad + 4])
-        load_a(0, 2)
-        load_a(0, 3)
-        x_raw = {}
-        x_view = x_words.bitcast(I32)
+        load_rows("a0", 0)
+        load_rows("a0", 1)
+        x_scale_view = x_scales.bitcast(I32).rearrange("g q w -> q g w")
+        for n in range(4):
+            nc.sync.dma_start(out=x_scale_raw[32 * n : 32 * n + 4, :, :], in_=x_scale_view[4 * n : 4 * n + 4])
+        load_rows("a0", 2)
+        load_rows("a0", 3)
+        x_raw = keep.tile([P, G, 512], I32, name="x_raw")
         for g in range(G):
-            x_raw[g] = keep.tile([P, 512], I32, name="x_raw_%d" % g)
-            nc.sync.dma_start(out=x_raw[g][:], in_=x_view[g])
+            nc.sync.dma_start(out=x_raw[:, g, :], in_=x_words.bitcast(I32)[g])
+        lam_view = lam.rearrange("(h q t r) -> h t q r", h=H, t=T, r=8)
         for h in range(H):
-            nc.sync.dma_start(out=rows[4 * h : 4 * h + 4, :].rearrange("t (q r) -> t q r", r=8), in_=lam_view[h])
-        nc.sync.dma_start(out=rows[8:10, :], in_=lam_left.rearrange("(s p) -> s p", p=P))
-        nc.sync.dma_start(out=b_cols[:], in_=b_scale.rearrange("(g p t) o u -> p g (t o u)", p=P, t=4))
-
-        b_raw = keep.tile([P, G, 4096], U8, name="b_raw")
-        b_view = b_bytes.rearrange("(g p t) f j -> g p (t f j)", p=P, t=4)
+            rows = schmidt_rows[T * h : T * (h + 1), :]
+            nc.sync.dma_start(out=rows.rearrange("t (q r) -> t q r", r=8), in_=lam_view[h])
+        nc.sync.dma_start(out=schmidt_rows[8:10, :], in_=lam_left.rearrange("(s p) -> s p", p=P))
+        b_scale_cols = keep.tile([P, G, T], F32, name="b_scale_cols")
+        nc.sync.dma_start(out=b_scale_cols[:], in_=b_scale.rearrange("(g p t) o u -> p g (t o u)", p=P, t=T))
+        b_raw = keep.tile([P, G, T * 1024], U8, name="b_raw")
+        b_view = b_bytes.rearrange("(g p t) f j -> g p (t f j)", p=P, t=T)
         for g in range(G):
             nc.sync.dma_start(out=b_raw[:, g, :], in_=b_view[g])
-        for h in range(H):
-            for t in range(4):
-                load_y(h, t)
-        for e in range(4):
-            load_a(1, e)
-        right_bf = keep.tile([P, 256], BF16, name="right_bf")
-        nc.sync.dma_start(out=right_bf[:], in_=lam_right.partition_broadcast(P))
-        right = keep.tile([P, 2, 256], F32, name="right")
+        for operand in ("y0", "y1", "a1"):
+            for i in range(4):
+                load_rows(operand, i)
+        lam_right_bf = keep.tile([P, 256], BF16, name="lam_right_bf")
+        nc.sync.dma_start(out=lam_right_bf[:], in_=lam_right.partition_broadcast(P))
+        lam_right_twice = keep.tile([P, HALF], F32, name="lam_right_twice")
         for f in range(2):
-            nc.gpsimd.tensor_copy(out=right[:, f, :], in_=right_bf[:])
+            nc.gpsimd.tensor_copy(out=lam_right_twice[:, 256 * f : 256 * (f + 1)], in_=lam_right_bf[:])
 
-        x_codes = keep.tile([P, G, 4, H, 256], U8, name="x_codes", align_bytes=64)
-        x_plane = keep.tile([P, 4, G, H, 128], U8, name="x_plane", align_bytes=64)
-        codes = {}
-        planes = {}
-        for n in ("a0", "a1", "y0", "y1"):
-            codes[n] = keep.tile([P, G, 512], U32, name="codes_" + n, align_bytes=64)
-            planes[n] = keep.tile([P, G, 512], U8, name="planes_" + n, align_bytes=64)
-        for n in ("b0", "b1"):
-            codes[n] = keep.tile([P, G, 512], U32, name="codes_" + n, align_bytes=64)
-            planes[n] = keep.tile([P, G, 512], U8, name="planes_" + n, align_bytes=64)
-        for n in ("l0", "l1", "r0", "r1"):
-            codes[n] = keep.tile([P, H, 512], U32, name="codes_" + n, align_bytes=64)
-            planes[n] = keep.tile([P, H, 512], U8, name="planes_" + n, align_bytes=64)
+        codes, scales = {}, {}
+        for operand in ("a0", "a1", "y0", "y1", "b0", "b1", "l0", "l1", "r0", "r1"):
+            passes = H if operand[0] in "lr" else G
+            codes[operand] = keep.tile([P, passes, HALF], U32, name="codes_" + operand, align_bytes=64)
+            scales[operand] = keep.tile([P, passes, HALF], U8, name="scales_" + operand, align_bytes=64)
+        x_codes = keep.tile([P, G, T, H, 256], U8, name="x_codes", align_bytes=64)
+        x_scale = keep.tile([P, T, G, H, 128], U8, name="x_scale", align_bytes=64)
 
-        def copy_out(engine, out_ap, in_ap):
+        def quantize(operand, g, source, lo=0, hi=HALF):
+            nc.vector.quantize_mx(
+                out=codes[operand][:, g, lo:hi].bitcast(FP8X4), scales=scales[operand][:, g, lo:hi], in_=source
+            )
+
+        def matmul(acc, stationary, moving, start, stop):
+            nc.tensor.matmul_mx(
+                out=acc,
+                lhsT=stationary[0],
+                lhsT_scale=stationary[1],
+                rhs=moving[0],
+                rhs_scale=moving[1],
+                start=start,
+                stop=stop,
+            )
+
+        def mx(operand, g, lo, hi):
+            return codes[operand][:, g, lo:hi].bitcast(FP8X4), scales[operand][:, g, lo:hi]
+
+        def bank(shape, dtype=F32):
+            return psum.tile(shape, dtype, name="bank", bufs=BANKS)
+
+        def copy(engine, dst, src):
             if engine == "S":
-                nc.scalar.copy(out=out_ap, in_=in_ap)
+                nc.scalar.copy(out=dst, in_=src)
             else:
-                nc.vector.tensor_copy(out=out_ap, in_=in_ap)
-
-        grouped = {}
-
-        sorted_words = {}
-
-        def sort_words(n, e, engine):
-            raw = (a_raw if n[0] == "a" else y_raw)[int(n[1]), e]
-            sorted_words[n, e] = stream.tile([P, G, 2, 128], F32, name="sorted", bufs=4)
-            copy_out(engine, sorted_words[n, e][:], raw[:].bitcast(F32).rearrange("p (g w u) -> p g u w", g=G, u=2))
+                nc.vector.tensor_copy(out=dst, in_=src)
 
         turned = {}
+        paired = {}
 
-        def transpose_words(acc, n, pair, x, g):
-            e = 2 * pair + x
-            raw = (a_raw if n[0] == "a" else y_raw)[int(n[1]), e]
+        def turn_tile(operand, i, g):
+            if i % 2 == 0:
+                turned[operand, i // 2, g] = bank([P, 2, 256])
+            acc = turned[operand, i // 2, g]
+            words = row_tiles[operand, i][:].bitcast(F32)
             for u in range(2):
-                if (n, e) in sorted_words:
-                    src = sorted_words[n, e][:, g, u, :]
+                src = words[:, 256 * g + u : 256 * (g + 1) : 2]
+                if operand[0] == "a":
+                    nc.tensor.transpose(acc[:, u, P * (i % 2) : P * (i % 2 + 1)], src, identity[:])
                 else:
-                    src = raw[:].bitcast(F32)[:, 256 * g + u : 256 * (g + 1) : 2]
-                if n[0] == "a":
-                    nc.tensor.transpose(acc[:, u, 128 * x : 128 * (x + 1)], src, ident[:])
-                else:
-                    nc.tensor.transpose(acc[:, u, :].rearrange("p (t x c) -> p x t c", t=4, x=2)[:, x], src, ident_y[:].rearrange("p t c -> p (t c)"))
+                    dst = acc[:, u, :].rearrange("p (t j c) -> p j t c", t=T, j=2)[:, i % 2]
+                    nc.tensor.transpose(dst, src, by_code[:])
 
-        def empty(n, pair, g, engine):
-            if (n, g) not in grouped:
-                grouped[n, g] = stream.tile([P, 2048], BF16, name="grouped", bufs=6, align_bytes=64)
-            acc = turned[n, pair, g]
-            dst = grouped[n, g][:].bitcast(F32)
-            if n[0] == "a":
-                dst = dst[:, 512 * pair : 512 * (pair + 1)].rearrange("p (c u) -> p c u", u=2)
-                copy_out(engine, dst, acc[:].rearrange("p u c -> p c u"))
+        def turn(operand, pair, g):
+            turn_tile(operand, 2 * pair, g)
+            turn_tile(operand, 2 * pair + 1, g)
+
+        def empty(operand, pair, g, engine):
+            if (operand, g) not in paired:
+                paired[operand, g] = stream.tile([P, T * HALF], BF16, name="paired", bufs=6, align_bytes=64)
+            words = paired[operand, g][:].bitcast(F32)
+            acc = turned[operand, pair, g]
+            if operand[0] == "a":
+                dst = words[:, 512 * pair : 512 * (pair + 1)].rearrange("p (c u) -> p c u", u=2)
+                copy(engine, dst, acc[:].rearrange("p u c -> p c u"))
             else:
-                dst = dst.rearrange("p (t x c u) -> p x t c u", t=4, x=2, u=2)[:, pair]
-                copy_out(engine, dst, acc[:].rearrange("p u (t c) -> p t c u", t=4))
+                dst = words.rearrange("p (t j c u) -> p j t c u", t=T, j=2, u=2)[:, pair]
+                copy(engine, dst, acc[:].rearrange("p u (t c) -> p t c u", t=T))
 
-        def turn(n, pair, g):
-            acc = psum.tile([P, 2, 256], F32, name="bank", bufs=8)
-            turned[n, pair, g] = acc
-            for x in range(2):
-                transpose_words(acc, n, pair, x, g)
+        def quantize_rows(operand, g, lo=0, hi=HALF):
+            quantize(operand, g, paired[operand, g][:, T * lo : T * hi], lo, hi)
 
-        def turn_tile(n, pair, x):
-            for g in range(G):
-                if x == 0:
-                    turned[n, pair, g] = psum.tile([P, 2, 256], F32, name="bank", bufs=8)
-            for g in range(G):
-                transpose_words(turned[n, pair, g], n, pair, x, g)
-
-        def warm_up():
-            warm_ps = psum.tile([P, 512], F32, name="bank", bufs=8)
-            for i in range(3):
-                nc.tensor.matmul(warm_ps[:], lhsT=ident_bf[:], rhs=warm[:], start=True, stop=True)
-
-        lam_cols = keep.tile([P, 10], F32, name="lam_cols")
-        lam_ps = {}
-
-        def lam_turn():
-            lam_ps[0] = psum.tile([P, P], BF16, name="bank", bufs=8)
-            nc.tensor.transpose(lam_ps[0][:], rows[:], ident_bf[:])
-
-        def lam_out():
-            nc.scalar.copy(out=lam_cols[:], in_=lam_ps[0][:, 0:10])
-
-        def quantize(n, c, lo=0, hi=512):
-            nc.vector.quantize_mx(out=codes[n][:, c, lo:hi].bitcast(FP8X4), scales=planes[n][:, c, lo:hi], in_=grouped[n, c][:, 4 * lo : 4 * hi])
-
-        def permute_scales():
+        def order_x_scales():
             nc.vector.tensor_copy(
-                out=x_plane[:].rearrange("p t g h c -> p (t g h c)").bitcast(I32).rearrange("p (t c r) -> p t c r", t=4, r=2),
-                in_=xs_raw[:].rearrange("p g w -> p (g w)").rearrange("p (c t r) -> p t c r", t=4, r=2),
+                out=x_scale[:].rearrange("p t g h c -> p (t g h c)").bitcast(I32).rearrange("p (t n w) -> p t n w", t=T, w=2),
+                in_=x_scale_raw[:].rearrange("p g w -> p (g w)").rearrange("p (n t w) -> p t n w", t=T, w=2),
             )
 
-        def permute_words(g):
+        def order_x_codes(g):
             nc.vector.tensor_copy(
-                out=x_codes[:, g].rearrange("p t h c -> p (t h c)").bitcast(I32).rearrange("p (t c r) -> p t c r", t=4, r=4),
-                in_=x_raw[g][:].rearrange("p (c t r) -> p t c r", t=4, r=4),
+                out=x_codes[:, g].rearrange("p t h c -> p (t h c)").bitcast(I32).rearrange("p (t n w) -> p t n w", t=T, w=4),
+                in_=x_raw[:, g, :].rearrange("p (n t w) -> p t n w", t=T, w=4),
             )
 
-        wide = [keep.tile([P, 4, 1024], BF16, name="wide_%d" % g, align_bytes=64) for g in range(G)]
+        b_wide = [keep.tile([P, T, 1024], BF16, name="b_wide_%d" % g, align_bytes=64) for g in range(G)]
 
-        def widen(g, t, half, engine):
-            lo = 512 * half
-            src = b_raw[:, g, 1024 * t + lo : 1024 * t + lo + 512].bitcast(FP8)
-            dst = wide[g][:, t, lo : lo + 512]
-            if engine == "S":
-                nc.scalar.activation(out=dst, in_=src, func=COPY, scale=b_cols[:, g, t : t + 1])
-            else:
-                nc.vector.tensor_scalar(out=dst, in0=src, scalar1=b_cols[:, g, t : t + 1], scalar2=None, op0=MULT)
+        def widen(engine, half, pieces):
+            for g, t in pieces:
+                lo = HALF * half
+                src = b_raw[:, g, 1024 * t + lo : 1024 * t + lo + HALF].bitcast(FP8)
+                dst = b_wide[g][:, t, lo : lo + HALF]
+                scale = b_scale_cols[:, g, t : t + 1]
+                if engine == "S":
+                    nc.scalar.activation(out=dst, in_=src, func=COPY, scale=scale)
+                else:
+                    nc.vector.tensor_scalar(out=dst, in0=src, scalar1=scale, scalar2=None, op0=MULT)
 
-        inter = {}
+        words_of = {}
 
         def interleave(key, src):
-            inter[key] = stream.tile([P, 512, 4], BF16, name="inter", bufs=4, align_bytes=64)
-            nc.vector.tensor_copy(out=inter[key][:].rearrange("p (c i) t -> p c t i", i=4), in_=src.rearrange("p t (c i) -> p c t i", i=4))
+            words_of[key] = stream.tile([P, HALF, T], BF16, name="words", bufs=4, align_bytes=64)
+            nc.vector.tensor_copy(
+                out=words_of[key][:].rearrange("p (c i) t -> p c t i", i=4),
+                in_=src.rearrange("p t (c i) -> p c t i", i=4),
+            )
 
-        def inter_flat(key):
-            return inter[key][:].rearrange("p n t -> p (n t)")
+        def interleave_b(g, half):
+            interleave(("b", g, half), b_wide[g][:, :, HALF * half : HALF * (half + 1)])
 
-        def b_inter(g, half):
-            interleave(("b", g, half), wide[g][:, :, 512 * half : 512 * (half + 1)])
+        def quantize_b(g, half):
+            quantize("b%d" % half, g, words_of["b", g, half][:].rearrange("p n t -> p (n t)"))
 
-        def b_quant(g, half):
-            nc.vector.quantize_mx(out=codes["b%d" % half][:, g, :].bitcast(FP8X4), scales=planes["b%d" % half][:, g, :], in_=inter_flat(("b", g, half)))
+        schmidt = keep.tile([P, 10], F32, name="schmidt")
+
+        def turn_schmidt():
+            acc = bank([P, P], BF16)
+            nc.tensor.transpose(acc[:], schmidt_rows[:], identity_bf[:])
+            nc.scalar.copy(out=schmidt[:], in_=acc[:, 0:10])
 
         l_acc = {}
         l_wide = {}
 
-        def l_mm(s, h):
-            for t in range(4):
-                l_acc[s, h, t] = psum.tile([P, 512], F32, name="bank", bufs=8)
-            n = "a%d" % s
+        def multiply_l(s, h):
+            for t in range(T):
+                l_acc[s, h, t] = bank([P, HALF])
             for g in range(G):
-                for t in range(4):
-                    nc.tensor.matmul_mx(
-                        out=l_acc[s, h, t][:],
-                        lhsT=x_codes[:, g, t, h, :].bitcast(FP4X4),
-                        lhsT_scale=x_plane[:, t, g, h, :],
-                        rhs=codes[n][:, g, :].bitcast(FP8X4),
-                        rhs_scale=planes[n][:, g, :],
-                        start=(g == 0),
-                        stop=(g == G - 1),
-                    )
+                for t in range(T):
+                    x = x_codes[:, g, t, h, :].bitcast(FP4X4), x_scale[:, t, g, h, :]
+                    matmul(l_acc[s, h, t][:], x, mx("a%d" % s, g, 0, HALF), g == 0, g == G - 1)
 
-        def l_out(s, h, t, engine):
-            if (s, h) not in l_wide:
-                l_wide[s, h] = stream.tile([P, 4, 512], BF16, name="l_wide", bufs=3, align_bytes=64)
-            scale = lam_cols[:, 4 * h + t : 4 * h + t + 1]
-            if engine == "S":
-                nc.scalar.activation(out=l_wide[s, h][:, t, :], in_=l_acc[s, h, t][:], func=COPY, scale=scale)
-            else:
-                nc.vector.tensor_scalar(out=l_wide[s, h][:, t, :], in0=l_acc[s, h, t][:], scalar1=scale, scalar2=None, op0=MULT)
+        def scale_l(s, h, first, engines):
+            for t, engine in enumerate(engines, first):
+                if t == 0:
+                    l_wide[s, h] = stream.tile([P, T, HALF], BF16, name="l_wide", bufs=3, align_bytes=64)
+                dst, scale = l_wide[s, h][:, t, :], schmidt[:, T * h + t : T * h + t + 1]
+                if engine == "S":
+                    nc.scalar.activation(out=dst, in_=l_acc[s, h, t][:], func=COPY, scale=scale)
+                else:
+                    nc.vector.tensor_scalar(out=dst, in0=l_acc[s, h, t][:], scalar1=scale, scalar2=None, op0=MULT)
 
-        def l_inter(s, h):
+        def interleave_l(s, h):
             interleave(("l", s, h), l_wide[s, h][:])
 
-        def l_quant(s, h):
-            n = "l%d" % s
-            nc.vector.quantize_mx(out=codes[n][:, h, :].bitcast(FP8X4), scales=planes[n][:, h, :], in_=inter_flat(("l", s, h)))
-
-        r_group = {}
+        def quantize_l(s, h):
+            quantize("l%d" % s, h, words_of["l", s, h][:].rearrange("p n t -> p (n t)"))
 
         r_acc = {}
+        r_words = {}
 
-        def r_mm(h, m, b):
-            acc = psum.tile([P, 2, 256], F32, name="bank", bufs=8)
-            r_acc[h, m, b] = acc
-            half, lo = m // 2, 256 * (m % 2)
-            yn, bn = "y%d" % h, "b%d" % half
-            for i in range(2):
-                t = 2 * b + i
+        def multiply_r(h, half, quarter):
+            acc = bank([P, 2, 256])
+            r_acc[h, half, quarter] = acc
+            lo = 256 * (quarter // 2)
+            for j in range(2):
+                t = 2 * (quarter % 2) + j
                 for g in range(G):
-                    nc.tensor.matmul_mx(
-                        out=acc[:, i, :],
-                        lhsT=codes[yn][:, g, 128 * t : 128 * (t + 1)].bitcast(FP8X4),
-                        lhsT_scale=planes[yn][:, g, 128 * t : 128 * (t + 1)],
-                        rhs=codes[bn][:, g, lo : lo + 256].bitcast(FP8X4),
-                        rhs_scale=planes[bn][:, g, lo : lo + 256],
-                        start=(g == 0),
-                        stop=(g == G - 1),
-                    )
+                    stationary = mx("y%d" % h, g, P * t, P * (t + 1))
+                    matmul(acc[:, j, :], stationary, mx("b%d" % half, g, lo, lo + 256), g == 0, g == G - 1)
 
-        def r_out(h, m, b, engine):
-            half, lo = m // 2, 256 * (m % 2)
-            if (h, half) not in r_group:
-                r_group[h, half] = stream.tile([P, 512, 4], BF16, name="r_group", bufs=3, align_bytes=64)
-            copy_out(engine, r_group[h, half][:, lo : lo + 256, 2 * b : 2 * b + 2], r_acc[h, m, b][:].rearrange("p t n -> p n t"))
+        def empty_r(h, half, quarter, engine):
+            if (h, half) not in r_words:
+                r_words[h, half] = stream.tile([P, HALF, T], BF16, name="r_words", bufs=3, align_bytes=64)
+            lo, t = 256 * (quarter // 2), 2 * (quarter % 2)
+            src = r_acc[h, half, quarter][:].rearrange("p j n -> p n j")
+            copy(engine, r_words[h, half][:, lo : lo + 256, t : t + 2], src)
 
-        def r_quant(h, half):
-            n = "r%d" % half
-            nc.vector.quantize_mx(out=codes[n][:, h, :].bitcast(FP8X4), scales=planes[n][:, h, :], in_=r_group[h, half][:].rearrange("p n t -> p (n t)"))
+        def quantize_r(h, half):
+            quantize("r%d" % half, h, r_words[h, half][:].rearrange("p n t -> p (n t)"))
 
-        out_view = out.rearrange("(s p e) n -> s e p n", p=P, e=4)
+        out_view = out.rearrange("(s p e) n -> s e p n", p=P, e=E)
 
-        t_acc = {}
-
-        def theta(s, e, half):
-            acc = psum.tile([P, 512], F32, name="bank", bufs=8)
-            ln, rn = "l%d" % s, "r%d" % half
+        def theta(s, e, half, stores=1):
+            acc = bank([P, HALF])
             for h in range(H):
-                nc.tensor.matmul_mx(
-                    out=acc[:],
-                    lhsT=codes[ln][:, h, 128 * e : 128 * (e + 1)].bitcast(FP8X4),
-                    lhsT_scale=planes[ln][:, h, 128 * e : 128 * (e + 1)],
-                    rhs=codes[rn][:, h, :].bitcast(FP8X4),
-                    rhs_scale=planes[rn][:, h, :],
-                    start=(h == 0),
-                    stop=(h == H - 1),
+                matmul(acc[:], mx("l%d" % s, h, P * e, P * (e + 1)), mx("r%d" % half, h, 0, HALF), h == 0, h == H - 1)
+            width = HALF // stores
+            for lo in range(0, HALF, width):
+                done = stream.tile([P, HALF], F32, name="done", tag="row_tile", bufs=10)
+                nc.vector.scalar_tensor_tensor(
+                    out=done[:, 0:width],
+                    in0=acc[:, lo : lo + width],
+                    scalar=schmidt[:, 8 + s : 9 + s],
+                    in1=lam_right_twice[:, lo : lo + width],
+                    op0=MULT,
+                    op1=MULT,
                 )
-            t_acc[s, e, half] = acc
+                nc.sync.dma_start(
+                    out=out_view[s, e][:, HALF * half + lo : HALF * half + lo + width], in_=done[:, 0:width]
+                )
 
-        def theta_out(s, e, half, parts=1):
-            acc = t_acc[s, e, half]
-            width = 512 // parts
-            for i in range(parts):
-                lo = width * i
-                o = stream.tile([P, 512], F32, name="o", tag="row_tile", bufs=10)
-                nc.vector.scalar_tensor_tensor(out=o[:, 0:width], in0=acc[:, lo : lo + width], scalar=lam_cols[:, 8 + s : 9 + s], in1=right[:].rearrange("p f j -> p (f j)")[:, lo : lo + width], op0=MULT, op1=MULT)
-                nc.sync.dma_start(out=out_view[s, e][:, 512 * half + lo : 512 * half + lo + width], in_=o[:, 0:width])
 
-        turn_tile("a0", 0, 0)
-        turn_tile("a0", 0, 1)
-        turn_tile("a0", 1, 0)
-        turn_tile("a0", 1, 1)
-        empty("a0", 0, 1, "S")
-        permute_scales()
-        empty("a0", 1, 0, "S")
-        empty("a0", 1, 1, "S")
-        empty("a0", 0, 2, "S")
-        empty("a0", 0, 0, "V")
-        quantize("a0", 0, 0, 256)
-        warm_up()
-        widen(0, 0, 1, "S")
-        quantize("a0", 1, 0, 256)
-        widen(0, 1, 0, "S")
-        permute_words(0)
-        empty("a0", 1, 2, "V")
-        quantize("a0", 0, 256, 512)
-        lam_turn()
-        lam_out()
-        quantize("a0", 1, 256, 512)
-        permute_words(1)
-        quantize("a0", 2, 256, 512)
-        quantize("a0", 2, 0, 256)
-        permute_words(2)
-        widen(0, 2, 0, "V")
-        widen(0, 0, 0, "V")
-        l_mm(0, 0)
-        l_mm(0, 1)
-        l_out(0, 0, 1, "S")
-        widen(1, 3, 0, "V")
-        l_out(0, 0, 2, "S")
-        widen(2, 2, 0, "S")
-        widen(1, 0, 0, "V")
-        widen(2, 3, 0, "S")
-        widen(1, 2, 0, "V")
-        l_out(0, 0, 3, "S")
-        widen(0, 3, 1, "V")
-        widen(1, 2, 1, "V")
-        widen(1, 1, 0, "V")
-        l_out(0, 0, 0, "V")
-        turn("y0", 0, 2)
-        widen(2, 0, 0, "V")
-        turn("y0", 1, 2)
-        widen(2, 1, 0, "S")
-        widen(0, 1, 1, "V")
-        l_out(0, 1, 0, "S")
-        l_out(0, 1, 2, "S")
-        l_out(0, 1, 1, "S")
-        turn("y0", 0, 1)
-        widen(2, 3, 1, "V")
-        turn("y0", 1, 0)
-        l_out(0, 1, 3, "S")
-        widen(0, 3, 0, "S")
-        turn("y1", 0, 1)
-        b_inter(1, 0)
-        turn("y0", 0, 0)
-        turn("y0", 1, 1)
-        empty("y0", 1, 0, "S")
-        empty("y0", 0, 2, "S")
-        turn("y1", 0, 2)
-        b_inter(2, 0)
-        empty("y0", 1, 2, "S")
-        empty("y0", 0, 1, "V")
-        empty("y0", 1, 1, "S")
-        b_quant(2, 0)
-        empty("y1", 0, 1, "V")
-        turn("y1", 1, 2)
-        b_inter(0, 0)
-        empty("y0", 0, 0, "S")
-        turn("y1", 1, 1)
-        turn("a1", 0, 2)
-        turn("y1", 0, 0)
-        quantize("y0", 2)
-        empty("y1", 1, 2, "V")
-        empty("y1", 0, 2, "S")
-        widen(1, 3, 1, "V")
-        b_quant(1, 0)
-        turn("a1", 0, 0)
-        widen(2, 0, 1, "S")
-        b_quant(0, 0)
-        widen(2, 2, 1, "S")
-        turn("a1", 0, 1)
-        turn("a1", 1, 2)
-        empty("y1", 1, 1, "S")
-        widen(0, 2, 1, "S")
-        quantize("y0", 0)
-        turn("a1", 1, 0)
-        turn("a1", 1, 1)
-        quantize("y0", 1)
-        empty("a1", 0, 2, "S")
-        empty("y1", 0, 0, "V")
-        empty("a1", 0, 0, "V")
-        quantize("y1", 1)
-        empty("a1", 1, 0, "S")
-        quantize("a1", 0)
-        empty("a1", 1, 1, "S")
-        turn("y1", 1, 0)
-        empty("a1", 1, 2, "S")
-        empty("a1", 0, 1, "S")
-        b_inter(0, 1)
-        quantize("a1", 1)
-        empty("y1", 1, 0, "S")
-        r_mm(0, 1, 0)
-        r_mm(0, 0, 0)
-        r_out(0, 1, 0, "S")
-        r_out(0, 0, 0, "S")
-        r_mm(0, 1, 1)
-        widen(1, 1, 1, "S")
-        quantize("a1", 2)
-        l_inter(0, 0)
-        b_quant(0, 1)
-        quantize("y1", 0)
-        r_out(0, 1, 1, "S")
-        r_mm(0, 0, 1)
-        l_mm(1, 0)
-        widen(2, 1, 1, "S")
-        r_out(0, 0, 1, "S")
-        b_inter(2, 1)
-        l_mm(1, 1)
-        l_out(1, 0, 0, "V")
-        l_out(1, 0, 1, "S")
-        quantize("y1", 2)
-        r_quant(0, 0)
-        widen(1, 0, 1, "S")
-        r_mm(1, 1, 1)
-        b_inter(1, 1)
-        l_out(1, 0, 2, "S")
-        l_out(1, 0, 3, "S")
-        r_mm(1, 0, 0)
-        b_quant(2, 1)
-        b_quant(1, 1)
-        r_mm(1, 0, 1)
-        l_out(1, 1, 2, "S")
-        l_quant(0, 0)
-        r_mm(1, 3, 1)
-        l_out(1, 1, 0, "S")
-        l_inter(1, 0)
-        l_inter(0, 1)
-        r_mm(1, 1, 0)
-        l_out(1, 1, 1, "S")
-        r_mm(1, 2, 0)
-        l_out(1, 1, 3, "S")
-        r_mm(0, 3, 0)
-        r_out(1, 0, 0, "S")
-        r_mm(1, 3, 0)
-        r_out(1, 0, 1, "S")
-        r_out(1, 3, 1, "S")
-        r_out(1, 1, 1, "S")
-        l_inter(1, 1)
-        r_mm(1, 2, 1)
-        r_out(1, 1, 0, "S")
-        l_quant(1, 0)
-        r_mm(0, 2, 1)
-        r_quant(1, 0)
-        r_out(1, 2, 0, "S")
-        l_quant(0, 1)
-        l_quant(1, 1)
-        r_out(1, 3, 0, "S")
-        r_mm(0, 3, 1)
-        theta(0, 2, 0)
-        r_out(0, 3, 0, "S")
-        theta_out(0, 2, 0)
-        theta(0, 3, 0)
-        r_out(1, 2, 1, "S")
-        theta(1, 2, 0)
-        theta(1, 1, 0)
-        r_out(0, 2, 1, "S")
-        r_mm(0, 2, 0)
-        theta_out(0, 3, 0)
-        r_out(0, 3, 1, "S")
-        theta_out(1, 2, 0)
-        r_out(0, 2, 0, "S")
-        theta(0, 1, 0)
-        r_quant(1, 1)
-        theta_out(1, 1, 0)
-        theta(1, 3, 0)
-        theta_out(0, 1, 0)
-        r_quant(0, 1)
-        theta(1, 0, 0)
-        theta(0, 0, 0)
-        theta(1, 2, 1)
-        theta_out(1, 3, 0)
-        theta_out(0, 0, 0)
-        theta(0, 3, 1)
-        theta(0, 2, 1)
-        theta_out(1, 0, 0)
-        theta(1, 1, 1)
-        theta(0, 0, 1)
-        theta(1, 0, 1)
-        theta_out(0, 3, 1)
-        theta_out(1, 2, 1)
-        theta_out(1, 1, 1)
-        theta_out(0, 0, 1)
-        theta(0, 1, 1)
-        theta_out(1, 0, 1)
-        theta(1, 3, 1)
-        theta_out(0, 2, 1)
-        theta_out(1, 3, 1)
-        theta_out(0, 1, 1, parts=2)
+        for pair, engines in enumerate(("VSS", "SSV")):
+            for i in (2 * pair, 2 * pair + 1):
+                for g in range(G):
+                    turn_tile("a0", i, g)
+            if pair == 0:
+                order_x_scales()
+                for g in range(G):
+                    empty("a0", 0, g, engines[g])
+                for g in range(G):
+                    quantize_rows("a0", g, 0, 256)
+            else:
+                warm = bank([P, HALF])
+                for n in range(3):
+                    nc.tensor.matmul(warm[:], lhsT=identity_bf[:], rhs=zeros[:], start=True, stop=True)
+                for g in range(G):
+                    empty("a0", 1, g, engines[g])
+                for g in range(G):
+                    order_x_codes(g)
+                    quantize_rows("a0", g, 256, HALF)
+        turn_schmidt()
+
+        multiply_l(0, 0)
+        multiply_l(0, 1)
+        widen("V", 0, [(0, 0), (0, 2), (1, 0), (1, 1), (1, 2), (1, 3), (2, 0)])
+        widen("V", 1, [(0, 1), (0, 3), (1, 2), (2, 3)])
+        widen("S", 1, [(0, 0)])
+        widen("S", 0, [(0, 1), (0, 3)])
+        scale_l(0, 0, 0, "SS")
+        widen("S", 0, [(2, 1), (2, 2), (2, 3)])
+        scale_l(0, 0, 2, "SV")
+        scale_l(0, 1, 0, "SSSS")
+        for g in (1, 2, 0):
+            interleave_b(g, 0)
+
+        for n, engine in enumerate("SSSSVS"):
+            turn("y0", n // G, n % G)
+            empty("y0", n // G, n % G, engine)
+        quantize_b(1, 0)
+        quantize_b(2, 0)
+        quantize_rows("y0", 0)
+        for n, engine in enumerate("SVSSSV"):
+            turn("y1", n // G, n % G)
+            empty("y1", n // G, n % G, engine)
+            if n == 1:
+                quantize_b(0, 0)
+                quantize_rows("y0", 1)
+                quantize_rows("y0", 2)
+        widen("V", 1, [(1, 3)])
+        for n, engine in enumerate("VSSSSS"):
+            turn("a1", n // G, n % G)
+            empty("a1", n // G, n % G, engine)
+            if n == 0:
+                widen("S", 1, [(0, 2)])
+            elif n == 1:
+                interleave_b(0, 1)
+            elif n == 2:
+                widen("S", 1, [(2, 0)])
+            elif n == 3:
+                quantize_rows("y1", 0)
+            elif n == 4:
+                widen("S", 1, [(2, 2)])
+        quantize_rows("a1", 0)
+        quantize_rows("a1", 1)
+        interleave_l(0, 0)
+        quantize_rows("a1", 2)
+        quantize_b(0, 1)
+
+        for quarter in range(4):
+            multiply_r(0, 0, quarter)
+            empty_r(0, 0, quarter, "S")
+            if quarter > 0:
+                widen("S", 1, [((1, 1), (2, 1), (1, 0))[quarter - 1]])
+        quantize_rows("y1", 1)
+        quantize_rows("y1", 2)
+        interleave_b(2, 1)
+        multiply_l(1, 0)
+        quantize_r(0, 0)
+        quantize_l(0, 0)
+        scale_l(1, 0, 0, "VSSS")
+        multiply_l(1, 1)
+        scale_l(1, 1, 0, "SSSS")
+        interleave_b(1, 1)
+        quantize_b(2, 1)
+        quantize_b(1, 1)
+
+        for quarter in range(4):
+            multiply_r(1, 0, quarter)
+            empty_r(1, 0, quarter, "S")
+        interleave_l(1, 0)
+        interleave_l(0, 1)
+        quantize_l(1, 0)
+        quantize_l(0, 1)
+        interleave_l(1, 1)
+        for quarter in range(4):
+            multiply_r(1, 1, quarter)
+            empty_r(1, 1, quarter, "S")
+        quantize_r(1, 0)
+        quantize_l(1, 1)
+
+        blocks = [(s, e, half) for half in range(2) for s in range(2) for e in range(E)]
+        for quarter in range(2):
+            multiply_r(0, 1, quarter)
+            empty_r(0, 1, quarter, "S")
+        for n, (s, e, half) in enumerate(blocks):
+            theta(s, e, half, stores=2 if n == len(blocks) - 1 else 1)
+            if n == 1:
+                multiply_r(0, 1, 2)
+                empty_r(0, 1, 2, "V")
+            elif n == 2:
+                multiply_r(0, 1, 3)
+                empty_r(0, 1, 3, "S")
+                quantize_r(1, 1)
+            elif n == 5:
+                quantize_r(0, 1)

from contextlib import ExitStack

import concourse.mybir as mybir
from concourse.masks import make_identity

FLOPS = 2 * 1024 * 1536 * 1024 * 2 + 2 * 1024 * 1024 * 1024

F32 = mybir.dt.float32
BF16 = mybir.dt.bfloat16
I32 = mybir.dt.int32
U32 = mybir.dt.uint32
U8 = mybir.dt.uint8
FP8 = mybir.dt.float8_e4m3fn
FP8X4 = mybir.dt.float8_e4m3fn_x4
FP4X4 = mybir.dt.float4_e2m1fn_x4
COPY = mybir.ActivationFunctionType.Copy
MULT = mybir.AluOpType.mult

P = 128
OLD = 1536
G = 3
H = 2
T = 4
E = 4
HALF = 512
BANKS = 8


def tile_two_site_tensor_s11_kernel(
    tc, a, x_words, x_scales, y, b_bytes, b_scale, lam, lam_left, lam_right, out
):
    nc = tc.nc
    with ExitStack() as ctx:
        keep = ctx.enter_context(tc.tile_pool(name="keep", bufs=1))
        stream = ctx.enter_context(tc.tile_pool(name="stream", bufs=2))
        psum = ctx.enter_context(tc.psum_pool(name="psum", bufs=BANKS))
        ctx.enter_context(tc.manual_schedule())

        identity = keep.tile([P, P], F32, name="identity")
        make_identity(nc, identity[:])
        by_code = keep.tile([P, P], F32, name="by_code")
        nc.gpsimd.tensor_copy(
            out=by_code[:].rearrange("p (t q r) -> p t q r", t=T, r=8),
            in_=identity[:].rearrange("p (q t r) -> p t q r", t=T, r=8),
        )
        identity_bf = keep.tile([P, P], BF16, name="identity_bf")
        make_identity(nc, identity_bf[:])
        zeros = keep.tile([P, HALF], BF16, name="zeros")
        nc.gpsimd.memset(zeros[:], 0.0)

        x_scale_raw = keep.tile([P, G, 256], I32, name="x_scale_raw")
        nc.vector.memset(x_scale_raw[:], 0)
        schmidt_rows = keep.tile([P, P], BF16, name="schmidt_rows")
        nc.vector.memset(schmidt_rows[:], 0.0)

        a_view = a.rearrange("(s p) e k -> s e p k", p=P)
        y_view = y.rearrange("(h j p) k -> h j p k", h=H, p=P)
        row_tiles = {}

        def load_rows(operand, i):
            view = a_view if operand[0] == "a" else y_view
            row_tiles[operand, i] = stream.tile([P, OLD], BF16, name="row_tile", bufs=10)
            nc.sync.dma_start(out=row_tiles[operand, i][:], in_=view[int(operand[1]), i])

        load_rows("a0", 0)
        load_rows("a0", 1)
        x_scale_view = x_scales.bitcast(I32).rearrange("g q w -> q g w")
        for n in range(4):
            nc.sync.dma_start(out=x_scale_raw[32 * n : 32 * n + 4, :, :], in_=x_scale_view[4 * n : 4 * n + 4])
        load_rows("a0", 2)
        load_rows("a0", 3)
        x_raw = keep.tile([P, G, 512], I32, name="x_raw")
        for g in range(G):
            nc.sync.dma_start(out=x_raw[:, g, :], in_=x_words.bitcast(I32)[g])
        lam_view = lam.rearrange("(h q t r) -> h t q r", h=H, t=T, r=8)
        for h in range(H):
            rows = schmidt_rows[T * h : T * (h + 1), :]
            nc.sync.dma_start(out=rows.rearrange("t (q r) -> t q r", r=8), in_=lam_view[h])
        nc.sync.dma_start(out=schmidt_rows[8:10, :], in_=lam_left.rearrange("(s p) -> s p", p=P))
        b_scale_cols = keep.tile([P, G, T], F32, name="b_scale_cols")
        nc.sync.dma_start(out=b_scale_cols[:], in_=b_scale.rearrange("(g p t) o u -> p g (t o u)", p=P, t=T))
        b_raw = keep.tile([P, G, T * 1024], U8, name="b_raw")
        b_view = b_bytes.rearrange("(g p t) f j -> g p (t f j)", p=P, t=T)
        for g in range(G):
            nc.sync.dma_start(out=b_raw[:, g, :], in_=b_view[g])
        for operand in ("y0", "y1", "a1"):
            for i in range(4):
                load_rows(operand, i)
        lam_right_bf = keep.tile([P, 256], BF16, name="lam_right_bf")
        nc.sync.dma_start(out=lam_right_bf[:], in_=lam_right.partition_broadcast(P))
        lam_right_twice = keep.tile([P, HALF], F32, name="lam_right_twice")
        for f in range(2):
            nc.gpsimd.tensor_copy(out=lam_right_twice[:, 256 * f : 256 * (f + 1)], in_=lam_right_bf[:])

        codes, scales = {}, {}
        for operand in ("a0", "a1", "y0", "y1", "b0", "b1", "l0", "l1", "r0", "r1"):
            passes = H if operand[0] in "lr" else G
            codes[operand] = keep.tile([P, passes, HALF], U32, name="codes_" + operand, align_bytes=64)
            scales[operand] = keep.tile([P, passes, HALF], U8, name="scales_" + operand, align_bytes=64)
        x_codes = keep.tile([P, G, T, H, 256], U8, name="x_codes", align_bytes=64)
        x_scale = keep.tile([P, T, G, H, 128], U8, name="x_scale", align_bytes=64)

        def quantize(operand, g, source, lo=0, hi=HALF):
            nc.vector.quantize_mx(
                out=codes[operand][:, g, lo:hi].bitcast(FP8X4), scales=scales[operand][:, g, lo:hi], in_=source
            )

        def matmul(acc, stationary, moving, start, stop):
            nc.tensor.matmul_mx(
                out=acc,
                lhsT=stationary[0],
                lhsT_scale=stationary[1],
                rhs=moving[0],
                rhs_scale=moving[1],
                start=start,
                stop=stop,
            )

        def mx(operand, g, lo, hi):
            return codes[operand][:, g, lo:hi].bitcast(FP8X4), scales[operand][:, g, lo:hi]

        def bank(shape, dtype=F32):
            return psum.tile(shape, dtype, name="bank", bufs=BANKS)

        def copy(engine, dst, src):
            if engine == "S":
                nc.scalar.copy(out=dst, in_=src)
            else:
                nc.vector.tensor_copy(out=dst, in_=src)

        turned = {}
        paired = {}

        def turn_tile(operand, i, g):
            if i % 2 == 0:
                turned[operand, i // 2, g] = bank([P, 2, 256])
            acc = turned[operand, i // 2, g]
            words = row_tiles[operand, i][:].bitcast(F32)
            for u in range(2):
                src = words[:, 256 * g + u : 256 * (g + 1) : 2]
                if operand[0] == "a":
                    nc.tensor.transpose(acc[:, u, P * (i % 2) : P * (i % 2 + 1)], src, identity[:])
                else:
                    dst = acc[:, u, :].rearrange("p (t j c) -> p j t c", t=T, j=2)[:, i % 2]
                    nc.tensor.transpose(dst, src, by_code[:])

        def turn(operand, pair, g):
            turn_tile(operand, 2 * pair, g)
            turn_tile(operand, 2 * pair + 1, g)

        def empty(operand, pair, g, engine):
            if (operand, g) not in paired:
                paired[operand, g] = stream.tile([P, T * HALF], BF16, name="paired", bufs=6, align_bytes=64)
            words = paired[operand, g][:].bitcast(F32)
            acc = turned[operand, pair, g]
            if operand[0] == "a":
                dst = words[:, 512 * pair : 512 * (pair + 1)].rearrange("p (c u) -> p c u", u=2)
                copy(engine, dst, acc[:].rearrange("p u c -> p c u"))
            else:
                dst = words.rearrange("p (t j c u) -> p j t c u", t=T, j=2, u=2)[:, pair]
                copy(engine, dst, acc[:].rearrange("p u (t c) -> p t c u", t=T))

        def quantize_rows(operand, g, lo=0, hi=HALF):
            quantize(operand, g, paired[operand, g][:, T * lo : T * hi], lo, hi)

        def order_x_scales():
            nc.vector.tensor_copy(
                out=x_scale[:].rearrange("p t g h c -> p (t g h c)").bitcast(I32).rearrange("p (t n w) -> p t n w", t=T, w=2),
                in_=x_scale_raw[:].rearrange("p g w -> p (g w)").rearrange("p (n t w) -> p t n w", t=T, w=2),
            )

        def order_x_codes(g):
            nc.vector.tensor_copy(
                out=x_codes[:, g].rearrange("p t h c -> p (t h c)").bitcast(I32).rearrange("p (t n w) -> p t n w", t=T, w=4),
                in_=x_raw[:, g, :].rearrange("p (n t w) -> p t n w", t=T, w=4),
            )

        b_wide = [keep.tile([P, T, 1024], BF16, name="b_wide_%d" % g, align_bytes=64) for g in range(G)]

        def widen(engine, half, pieces):
            for g, t in pieces:
                lo = HALF * half
                src = b_raw[:, g, 1024 * t + lo : 1024 * t + lo + HALF].bitcast(FP8)
                dst = b_wide[g][:, t, lo : lo + HALF]
                scale = b_scale_cols[:, g, t : t + 1]
                if engine == "S":
                    nc.scalar.activation(out=dst, in_=src, func=COPY, scale=scale)
                else:
                    nc.vector.tensor_scalar(out=dst, in0=src, scalar1=scale, scalar2=None, op0=MULT)

        words_of = {}

        def interleave(key, src):
            words_of[key] = stream.tile([P, HALF, T], BF16, name="words", bufs=4, align_bytes=64)
            nc.vector.tensor_copy(
                out=words_of[key][:].rearrange("p (c i) t -> p c t i", i=4),
                in_=src.rearrange("p t (c i) -> p c t i", i=4),
            )

        def interleave_b(g, half):
            interleave(("b", g, half), b_wide[g][:, :, HALF * half : HALF * (half + 1)])

        def quantize_b(g, half):
            quantize("b%d" % half, g, words_of["b", g, half][:].rearrange("p n t -> p (n t)"))

        schmidt = keep.tile([P, 10], F32, name="schmidt")

        def turn_schmidt():
            acc = bank([P, P], BF16)
            nc.tensor.transpose(acc[:], schmidt_rows[:], identity_bf[:])
            nc.scalar.copy(out=schmidt[:], in_=acc[:, 0:10])

        l_acc = {}
        l_wide = {}

        def multiply_l(s, h):
            for t in range(T):
                l_acc[s, h, t] = bank([P, HALF])
            for g in range(G):
                for t in range(T):
                    x = x_codes[:, g, t, h, :].bitcast(FP4X4), x_scale[:, t, g, h, :]
                    matmul(l_acc[s, h, t][:], x, mx("a%d" % s, g, 0, HALF), g == 0, g == G - 1)

        def scale_l(s, h, first, engines):
            for t, engine in enumerate(engines, first):
                if t == 0:
                    l_wide[s, h] = stream.tile([P, T, HALF], BF16, name="l_wide", bufs=3, align_bytes=64)
                dst, scale = l_wide[s, h][:, t, :], schmidt[:, T * h + t : T * h + t + 1]
                if engine == "S":
                    nc.scalar.activation(out=dst, in_=l_acc[s, h, t][:], func=COPY, scale=scale)
                else:
                    nc.vector.tensor_scalar(out=dst, in0=l_acc[s, h, t][:], scalar1=scale, scalar2=None, op0=MULT)

        def interleave_l(s, h):
            interleave(("l", s, h), l_wide[s, h][:])

        def quantize_l(s, h):
            quantize("l%d" % s, h, words_of["l", s, h][:].rearrange("p n t -> p (n t)"))

        r_acc = {}
        r_words = {}

        def multiply_r(h, half, quarter):
            acc = bank([P, 2, 256])
            r_acc[h, half, quarter] = acc
            lo = 256 * (quarter // 2)
            for j in range(2):
                t = 2 * (quarter % 2) + j
                for g in range(G):
                    stationary = mx("y%d" % h, g, P * t, P * (t + 1))
                    matmul(acc[:, j, :], stationary, mx("b%d" % half, g, lo, lo + 256), g == 0, g == G - 1)

        def empty_r(h, half, quarter, engine):
            if (h, half) not in r_words:
                r_words[h, half] = stream.tile([P, HALF, T], BF16, name="r_words", bufs=3, align_bytes=64)
            lo, t = 256 * (quarter // 2), 2 * (quarter % 2)
            src = r_acc[h, half, quarter][:].rearrange("p j n -> p n j")
            copy(engine, r_words[h, half][:, lo : lo + 256, t : t + 2], src)

        def quantize_r(h, half):
            quantize("r%d" % half, h, r_words[h, half][:].rearrange("p n t -> p (n t)"))

        out_view = out.rearrange("(s p e) n -> s e p n", p=P, e=E)

        def theta(s, e, half, stores=1):
            acc = bank([P, HALF])
            for h in range(H):
                matmul(acc[:], mx("l%d" % s, h, P * e, P * (e + 1)), mx("r%d" % half, h, 0, HALF), h == 0, h == H - 1)
            width = HALF // stores
            for lo in range(0, HALF, width):
                done = stream.tile([P, HALF], F32, name="done", tag="row_tile", bufs=10)
                nc.vector.scalar_tensor_tensor(
                    out=done[:, 0:width],
                    in0=acc[:, lo : lo + width],
                    scalar=schmidt[:, 8 + s : 9 + s],
                    in1=lam_right_twice[:, lo : lo + width],
                    op0=MULT,
                    op1=MULT,
                )
                nc.sync.dma_start(
                    out=out_view[s, e][:, HALF * half + lo : HALF * half + lo + width], in_=done[:, 0:width]
                )


        for pair, engines in enumerate(("VSS", "SSV")):
            for i in (2 * pair, 2 * pair + 1):
                for g in range(G):
                    turn_tile("a0", i, g)
            if pair == 0:
                order_x_scales()
                for g in range(G):
                    empty("a0", 0, g, engines[g])
                for g in range(G):
                    quantize_rows("a0", g, 0, 256)
            else:
                warm = bank([P, HALF])
                for n in range(3):
                    nc.tensor.matmul(warm[:], lhsT=identity_bf[:], rhs=zeros[:], start=True, stop=True)
                for g in range(G):
                    empty("a0", 1, g, engines[g])
                for g in range(G):
                    order_x_codes(g)
                    quantize_rows("a0", g, 256, HALF)
        turn_schmidt()

        multiply_l(0, 0)
        multiply_l(0, 1)
        widen("V", 0, [(0, 0), (0, 2), (1, 0), (1, 1), (1, 2), (1, 3), (2, 0)])
        widen("V", 1, [(0, 1), (0, 3), (1, 2), (2, 3)])
        widen("S", 1, [(0, 0)])
        widen("S", 0, [(0, 1), (0, 3)])
        scale_l(0, 0, 0, "SS")
        widen("S", 0, [(2, 1), (2, 2), (2, 3)])
        scale_l(0, 0, 2, "SV")
        scale_l(0, 1, 0, "SSSS")
        for g in (1, 2, 0):
            interleave_b(g, 0)

        for n, engine in enumerate("SSSSVS"):
            turn("y0", n // G, n % G)
            empty("y0", n // G, n % G, engine)
        quantize_b(1, 0)
        quantize_b(2, 0)
        quantize_rows("y0", 0)
        for n, engine in enumerate("SVSSSV"):
            turn("y1", n // G, n % G)
            empty("y1", n // G, n % G, engine)
            if n == 1:
                quantize_b(0, 0)
                quantize_rows("y0", 1)
                quantize_rows("y0", 2)
        widen("V", 1, [(1, 3)])
        for n, engine in enumerate("VSSSSS"):
            turn("a1", n // G, n % G)
            empty("a1", n // G, n % G, engine)
            if n == 0:
                widen("S", 1, [(0, 2)])
            elif n == 1:
                interleave_b(0, 1)
            elif n == 2:
                widen("S", 1, [(2, 0)])
            elif n == 3:
                quantize_rows("y1", 0)
            elif n == 4:
                widen("S", 1, [(2, 2)])
        quantize_rows("a1", 0)
        quantize_rows("a1", 1)
        interleave_l(0, 0)
        quantize_rows("a1", 2)
        quantize_b(0, 1)

        for quarter in range(4):
            multiply_r(0, 0, quarter)
            empty_r(0, 0, quarter, "S")
            if quarter > 0:
                widen("S", 1, [((1, 1), (2, 1), (1, 0))[quarter - 1]])
        quantize_rows("y1", 1)
        quantize_rows("y1", 2)
        interleave_b(2, 1)
        multiply_l(1, 0)
        quantize_r(0, 0)
        quantize_l(0, 0)
        scale_l(1, 0, 0, "VSSS")
        multiply_l(1, 1)
        scale_l(1, 1, 0, "SSSS")
        interleave_b(1, 1)
        quantize_b(2, 1)
        quantize_b(1, 1)

        for quarter in range(4):
            multiply_r(1, 0, quarter)
            empty_r(1, 0, quarter, "S")
        interleave_l(1, 0)
        interleave_l(0, 1)
        quantize_l(1, 0)
        quantize_l(0, 1)
        interleave_l(1, 1)
        for quarter in range(4):
            multiply_r(1, 1, quarter)
            empty_r(1, 1, quarter, "S")
        quantize_r(1, 0)
        quantize_l(1, 1)

        blocks = [(s, e, half) for half in range(2) for s in range(2) for e in range(E)]
        for quarter in range(2):
            multiply_r(0, 1, quarter)
            empty_r(0, 1, quarter, "S")
        for n, (s, e, half) in enumerate(blocks):
            theta(s, e, half, stores=2 if n == len(blocks) - 1 else 1)
            if n == 1:
                multiply_r(0, 1, 2)
                empty_r(0, 1, 2, "V")
            elif n == 2:
                multiply_r(0, 1, 3)
                empty_r(0, 1, 3, "S")
                quantize_r(1, 1)
            elif n == 5:
                quantize_r(0, 1)
